import numpy as np
import ml_dtypes


def mxq(x, axis, fmt="e4m3"):
    dtype, down = {"e4m3": (ml_dtypes.float8_e4m3fn, 7), "e5m2": (ml_dtypes.float8_e5m2, 14)}[fmt]
    v = np.moveaxis(np.asarray(x, np.float32).astype(ml_dtypes.bfloat16).astype(np.float64), axis, -1)
    blocks = v.reshape(v.shape[:-1] + (-1, 32))
    amax = np.abs(blocks).max(-1, keepdims=True)
    byte = np.maximum(np.where(amax > 0, np.frexp(amax)[1] - 1 + 127, 0) - down, 1)
    scale = np.exp2(byte - 127.0)
    codes = (blocks / scale).astype(np.float32).astype(dtype).astype(np.float64)
    return np.moveaxis((codes * scale).reshape(v.shape), -1, axis)


WIDE = False


def mx_kscale(k):
    if not WIDE:
        return np.ones(k)
    levels = np.array([10, -10, 5, -5, 0])
    if k % 512:
        return np.exp2(np.random.permutation(np.resize(levels, k // 32))).repeat(32)
    a = np.empty((k // 512, 16))
    for p in range(k // 512):
        a[p, :8] = np.random.permutation(np.resize(levels, 8))
        for g in range(8):
            far = levels[np.abs(levels - a[p, g]) >= 10]
            a[p, g + 8] = far[np.random.randint(len(far))]
    return np.exp2(a.ravel()).repeat(32)


def f64(x):
    return np.asarray(x).astype(np.float64)


def striped(idx):
    return np.tile(idx.reshape(-1, 16).T, (8, 1)).astype(np.uint16)


def unstriped(offs):
    return offs[:16].T.reshape(-1).astype(np.int64)


E2M1 = np.array([0.0, 0.5, 1.0, 1.5, 2.0, 3.0, 4.0, 6.0, -0.0, -0.5, -1.0, -1.5, -2.0, -3.0, -4.0, -6.0])


def pack_weight(w, fmt):
    k, n = w.shape
    w = f64(np.asarray(w, np.float32).astype(ml_dtypes.bfloat16)).reshape(k // 32, 32, n)
    amax = np.abs(w).max(1)
    if fmt == "e4m3":
        byte = np.frexp(amax)[1] - 1 + 127 - 7
    else:
        mant, ex = np.frexp(amax / 6.0)
        byte = np.where(mant > 0.5, ex, ex - 1) + 127
    byte = np.clip(np.where(amax > 0, byte, 1), 1, 254)
    scaled = (w * np.exp2(127.0 - byte)[:, None, :]).reshape(k, n).astype(np.float32)
    by_word = np.ascontiguousarray(scaled.reshape(k // 512, 128, 4, n).transpose(0, 1, 3, 2))
    if fmt == "e4m3":
        words = by_word.astype(ml_dtypes.float8_e4m3fn).view(np.uint8)
    else:
        c = by_word.astype(ml_dtypes.float4_e2m1fn).view(np.uint8) & 0xF
        words = (c[..., 0::2] | (c[..., 1::2] << 4)).reshape(k // 512, 128, 2 * n)
    return np.ascontiguousarray(words), np.ascontiguousarray(byte.astype(np.uint8).reshape(k // 512, 16, n))


def unpack_weight(words, scales, fmt):
    g, _, n = scales.shape
    words = np.ascontiguousarray(words).reshape(g, 128, n, -1)
    if fmt == "e4m3":
        vals = words.view(ml_dtypes.float8_e4m3fn).astype(np.float64)
    else:
        nib = np.empty((g, 128, n, 4), np.uint8)
        nib[..., 0::2] = words & 0xF
        nib[..., 1::2] = words >> 4
        vals = E2M1[nib]
    vals = vals * np.repeat(np.exp2(scales.astype(np.float64) - 127.0), 8, axis=1)[..., None]
    return vals.transpose(0, 1, 3, 2).reshape(g * 512, n)


def relu(v):
    return np.maximum(v, 0.0)


K, T, E, C, N = 1536, 1024, 12, 128, 256
R = 2


def by_expert(wq, xq):
    return np.concatenate([wq[e].T @ xq[:, e * C:(e + 1) * C] for e in range(E)], axis=1)


def setup_inputs():
    n = np.random.standard_normal
    s = mx_kscale(K)[:, None]
    slot_token = np.concatenate([r * (T // R) + np.random.permutation(T // R)[:C // R] for e in range(E) for r in range(R)])
    w = [pack_weight(m, "e2m1") for m in n((E, K, N)) / np.sqrt(K) / s[None]]
    return {
        "xT": (n((K, T)) * s).astype(np.float32),
        "w_words": np.stack([m[0] for m in w]),
        "w_scales": np.stack([m[1] for m in w]),
        "b": (0.3 * n((N, E))).astype(np.float32),
        "offs": striped(slot_token),
    }


def reference(xT, w_words, w_scales, b, offs):
    idx = unstriped(offs)
    w = np.stack([unpack_weight(w_words[e], w_scales[e], "e2m1") for e in range(E)])
    xq = mxq(f64(xT)[:, idx], 0, "e4m3")
    y = by_expert(w, xq)
    y = relu(y + np.repeat(f64(b), C, axis=1))
    return y.reshape(N, E, R, C // R).transpose(0, 2, 1, 3).reshape(N, E * C)

@@ -1,0 +1,148 @@
+import concourse.mybir as mybir
+
+FLOPS = 2 * 1536 * 1536 * 256
+
+K, T, E, C, N = 1536, 1024, 12, 128, 256
+P = 128
+PASSES = 3
+S = E * C
+F32 = mybir.dt.float32
+BF16 = mybir.dt.bfloat16
+I32 = mybir.dt.int32
+U32 = mybir.dt.uint32
+U16 = mybir.dt.uint16
+U8 = mybir.dt.uint8
+FP8X4 = mybir.dt.float8_e4m3fn_x4
+FP4X4 = mybir.dt.float4_e2m1fn_x4
+RELU = mybir.ActivationFunctionType.Relu
+
+ADD = mybir.AluOpType.add
+MAX = mybir.AluOpType.max
+LOADS = [(0, 0, 512), (0, 512, 512), (1, 0, 1024), (2, 0, 1024)]
+UNITS = [(0, 0, 512, 256), (1, 0, 512, 336), (2, 0, 512, 352), (2, 512, 512, 64), (3, 0, 512, 320), (3, 512, 512, 32)]
+WORDS = [(0, 0, 0, 512), (0, 1, 0, 512), (0, 2, 0, 512), (1, 0, 0, 512), (1, 1, 0, 512), (2, 0, 0, 512), (2, 1, 0, 512), (1, 2, 0, 512), (2, 2, 0, 256), (2, 2, 256, 256)]
+LATE = {(1, 2): "grp5"}
+BLOCKS = [4,4,4]
+STARTS = [sum(BLOCKS[:k]) for k in range(len(BLOCKS))]
+STORE_CUTS = [4,4,2,2]
+V_EVAC = 10
+LEAD = 4
+
+
+def tile_moe_eps_lin_relu_kernel(tc, xT, w_words, w_scales, b, offs, out):
+    nc = tc.nc
+    with (
+        tc.tile_pool(name="held", bufs=1) as held,
+        tc.psum_pool(name="psum", bufs=8) as psum,
+    ):
+        offsets = held.tile([P, S // 16], U16, name="offsets")
+        bias = held.tile([P, 2, E], F32, name="bias")
+        ws = held.tile([P, E * PASSES, N], U8, name="ws", align_bytes=64)
+        plane = held.tile([P, T], U8, name="plane", align_bytes=64)
+        codes = [held.tile([P, T], U32, name=f"codes{a}", align_bytes=64) for a in range(PASSES)]
+        ot = held.tile([P, 2, 2, E, 64], F32, name="ot", align_bytes=64)
+        block_of = [k for k, n in enumerate(BLOCKS) for i in range(n)]
+        wt = [held.tile([P, n * PASSES, 2 * N], U8, name=f"wt{k}", align_bytes=64) for k, n in enumerate(BLOCKS[:-1])]
+        sp = [
+            [held.tile([P, n * C], U8, name=f"sp{k}_{a}", align_bytes=64) for a in range(PASSES)] for k, n in enumerate(BLOCKS)
+        ]
+        warm = held.tile([P, 1], F32, name="warm")
+        nc.vector.memset(warm[:], 0)
+        nc.scalar.activation(out=warm[:], in_=warm[:], func=RELU)
+        nc.vector.memset(plane[:].bitcast(I32), 0)
+        nc.vector.memset(ws[:].rearrange("p g n -> p (g n)").bitcast(I32), 0)
+        for k in range(len(BLOCKS)):
+            for a in (1, 2):
+                nc.vector.memset(sp[k][a][:].bitcast(I32), 0)
+
+        raw = []
+        for i, (a, c0, w) in enumerate(LOADS):
+            r = held.tile([P, 4, w], F32, name=f"raw{i}", align_bytes=64)
+            nc.sync.dma_start(out=r[:], in_=xT[512 * a : 512 * a + 512, c0 : c0 + w].rearrange("(p j) w -> p j w", j=4))
+            raw.append(r)
+            if i == 1:
+                nc.sync.dma_start(offsets[:], offs)
+        ww = w_words.bitcast(I32).rearrange("e a p n -> p (e a) n")
+        wsc = w_scales.bitcast(I32).rearrange("e a q n -> q (e a) n")
+        for r in range(4):
+            nc.sync.dma_start(out=ws[r:P:32, :, :].bitcast(I32), in_=wsc[r:16:4])
+        def load_weights(k):
+            g0 = 3 * STARTS[k]
+            nc.sync.dma_start(out=wt[k][:].bitcast(I32), in_=ww[:, g0 : g0 + 3 * BLOCKS[k], :])
+
+        for k in range(len(BLOCKS) - 1):
+            load_weights(k)
+        nc.sync.dma_start(out=bias[:], in_=b.rearrange("(h p) e -> p h e", p=P))
+
+        def gather(dst, window, s0, n):
+            nc.vector.tensor_copy(dst, window[:].indirect(offsets[:, s0 // 16 : (s0 + n) // 16]))
+
+        for i, (load, off, w, v) in enumerate(UNITS):
+            a, c0 = LOADS[load][0], LOADS[load][1] + off
+            g = held.tile([P, w, 4], BF16, name=f"grp{i}", align_bytes=64)
+            src = raw[load][:].rearrange("p j w -> p w j")
+            if v < w:
+                nc.scalar.copy(out=g[:, v:w, :], in_=src[:, off + v : off + w, :])
+            if v > 0:
+                nc.vector.tensor_copy(out=g[:, 0:v, :], in_=src[:, off : off + v, :])
+            nc.vector.quantize_mx(
+                out=codes[a][:, c0 : c0 + w].bitcast(FP8X4),
+                scales=plane[4 * a : P, c0 : c0 + w],
+                in_=g[:].rearrange("p w j -> p (w j)"),
+            )
+        for k, n in enumerate(BLOCKS):
+            gather(sp[k][0][:], plane, C * STARTS[k], C * n)
+            for a in (1, 2):
+                nc.sync.dma_start(out=sp[k][a][0:112, :].bitcast(I32), in_=sp[k][0][4 * a : 112 + 4 * a, :].bitcast(I32))
+        wt.append(held.tile([P, BLOCKS[-1] * PASSES, 2 * N], U8, name="wt_last", tag="plane", align_bytes=64))
+        load_weights(len(BLOCKS) - 1)
+        gw = {}
+        for a, k, s0, n in WORDS:
+            if (a, k) not in gw:
+                gw[a, k] = held.tile(
+                    [P, C * BLOCKS[k]], U32, name=f"gw{a}_{k}", tag=LATE.get((a, k), f"gw{a}_{k}"), align_bytes=64
+                )
+            gather(gw[a, k][:, s0 : s0 + n], codes[a], C * STARTS[k] + s0, n)
+
+        def multiply(acc, e, h, a):
+            k = block_of[e]
+            i = e - STARTS[k]
+            nc.tensor.matmul_mx(
+                out=acc[:],
+                lhsT=wt[k][:, 3 * i + a, 256 * h : 256 * h + 256].bitcast(FP4X4),
+                lhsT_scale=ws[:, 3 * e + a, 128 * h : 128 * h + 128],
+                rhs=gw[a, k][:, C * i : C * i + C].bitcast(FP8X4),
+                rhs_scale=sp[k][a][:, C * i : C * i + C],
+                start=(a == 0),
+                stop=(a == PASSES - 1),
+            )
+
+        accs = {}
+        for e in range(LEAD):
+            for h in range(2):
+                accs[e, h] = psum.tile([P, C], F32, name="acc")
+        for a in range(2):
+            for e in range(LEAD):
+                for h in range(2):
+                    multiply(accs[e, h], e, h, a)
+        ov = out.rearrange("(h p) (m s) -> h p m s", p=P, m=2)
+        bounds = [sum(STORE_CUTS[:i]) for i in range(len(STORE_CUTS) + 1)]
+        for lo, hi in zip(bounds[:-1], bounds[1:]):
+            for e in range(lo, hi):
+                for h in range(2):
+                    if e < LEAD:
+                        acc = accs[e, h]
+                        multiply(acc, e, h, 2)
+                    else:
+                        acc = psum.tile([P, C], F32, name="acc")
+                        for a in range(PASSES):
+                            multiply(acc, e, h, a)
+                    res, sums = ot[:, h, :, e, :], acc[:].rearrange("p (m u) -> p m u", m=2)
+                    if e >= V_EVAC and h == 1:
+                        nc.vector.tensor_scalar(res, sums, bias[:, h, e : e + 1], 0.0, ADD, MAX)
+                    else:
+                        nc.scalar.activation(out=res, in_=sums, func=RELU, bias=bias[:, h, e : e + 1])
+            for h in range(2):
+                nc.sync.dma_start(
+                    out=ov[h, :, :, 64 * lo : 64 * hi], in_=ot[:, h, :, lo:hi, :].rearrange("p m e u -> p m (e u)")
+                )

@@ -16,17 +16,14 @@ FP8X4 = mybir.dt.float8_e4m3fn_x4
 FP4X4 = mybir.dt.float4_e2m1fn_x4
 RELU = mybir.ActivationFunctionType.Relu
 
+PIECES = [(0, 0, 512, 320), (0, 512, 512, 352), (1, 0, 512, 0), (1, 512, 512, 320), (2, 0, 512, 0), (2, 512, 256, 0), (2, 768, 256, 192)]
+G = 4
+BLOCKS = E // G
+W = G * C
+STORE_ENDS = (4, 8, 10, 12)
+VECTOR_FROM = 10
 ADD = mybir.AluOpType.add
 MAX = mybir.AluOpType.max
-LOADS = [(0, 0, 512), (0, 512, 512), (1, 0, 1024), (2, 0, 1024)]
-UNITS = [(0, 0, 512, 256), (1, 0, 512, 336), (2, 0, 512, 352), (2, 512, 512, 64), (3, 0, 512, 320), (3, 512, 512, 32)]
-WORDS = [(0, 0, 0, 512), (0, 1, 0, 512), (0, 2, 0, 512), (1, 0, 0, 512), (1, 1, 0, 512), (2, 0, 0, 512), (2, 1, 0, 512), (1, 2, 0, 512), (2, 2, 0, 256), (2, 2, 256, 256)]
-LATE = {(1, 2): "grp5"}
-BLOCKS = [4,4,4]
-STARTS = [sum(BLOCKS[:k]) for k in range(len(BLOCKS))]
-STORE_CUTS = [4,4,2,2]
-V_EVAC = 10
-LEAD = 4
 
 
 def tile_moe_eps_lin_relu_kernel(tc, xT, w_words, w_scales, b, offs, out):
@@ -41,108 +38,114 @@ def tile_moe_eps_lin_relu_kernel(tc, xT, w_words, w_scales, b, offs, out):
         plane = held.tile([P, T], U8, name="plane", align_bytes=64)
         codes = [held.tile([P, T], U32, name=f"codes{a}", align_bytes=64) for a in range(PASSES)]
         ot = held.tile([P, 2, 2, E, 64], F32, name="ot", align_bytes=64)
-        block_of = [k for k, n in enumerate(BLOCKS) for i in range(n)]
-        wt = [held.tile([P, n * PASSES, 2 * N], U8, name=f"wt{k}", align_bytes=64) for k, n in enumerate(BLOCKS[:-1])]
-        sp = [
-            [held.tile([P, n * C], U8, name=f"sp{k}_{a}", align_bytes=64) for a in range(PASSES)] for k, n in enumerate(BLOCKS)
-        ]
+        picked = [held.tile([P, W], U8, name=f"picked{k}", align_bytes=64) for k in range(BLOCKS)]
+        shifted = held.tile([P, 2 * S], U8, name="shifted", align_bytes=64)
+        wt = [held.tile([P, G * PASSES, 2 * N], U8, name=f"wt{k}", align_bytes=64) for k in range(BLOCKS)]
         warm = held.tile([P, 1], F32, name="warm")
         nc.vector.memset(warm[:], 0)
         nc.scalar.activation(out=warm[:], in_=warm[:], func=RELU)
         nc.vector.memset(plane[:].bitcast(I32), 0)
         nc.vector.memset(ws[:].rearrange("p g n -> p (g n)").bitcast(I32), 0)
-        for k in range(len(BLOCKS)):
-            for a in (1, 2):
-                nc.vector.memset(sp[k][a][:].bitcast(I32), 0)
+        nc.vector.memset(shifted[:].bitcast(I32), 0)
 
         raw = []
-        for i, (a, c0, w) in enumerate(LOADS):
+        for i, (a, c0, w, v) in enumerate(PIECES):
             r = held.tile([P, 4, w], F32, name=f"raw{i}", align_bytes=64)
             nc.sync.dma_start(out=r[:], in_=xT[512 * a : 512 * a + 512, c0 : c0 + w].rearrange("(p j) w -> p j w", j=4))
             raw.append(r)
-            if i == 1:
+            if i == 0:
                 nc.sync.dma_start(offsets[:], offs)
         ww = w_words.bitcast(I32).rearrange("e a p n -> p (e a) n")
         wsc = w_scales.bitcast(I32).rearrange("e a q n -> q (e a) n")
         for r in range(4):
             nc.sync.dma_start(out=ws[r:P:32, :, :].bitcast(I32), in_=wsc[r:16:4])
-        def load_weights(k):
-            g0 = 3 * STARTS[k]
-            nc.sync.dma_start(out=wt[k][:].bitcast(I32), in_=ww[:, g0 : g0 + 3 * BLOCKS[k], :])
 
-        for k in range(len(BLOCKS) - 1):
-            load_weights(k)
+        def load_weights(k):
+            nc.sync.dma_start(out=wt[k][:].bitcast(I32), in_=ww[:, G * PASSES * k : G * PASSES * (k + 1), :])
+
+        load_weights(0)
         nc.sync.dma_start(out=bias[:], in_=b.rearrange("(h p) e -> p h e", p=P))
 
-        def gather(dst, window, s0, n):
-            nc.vector.tensor_copy(dst, window[:].indirect(offsets[:, s0 // 16 : (s0 + n) // 16]))
+        def gather(dst, window, k, parts=1):
+            n = W // parts
+            for s0 in range(0, W, n):
+                lo = (k * W + s0) // 16
+                nc.vector.tensor_copy(dst[:, s0 : s0 + n], window[:].indirect(offsets[:, lo : lo + n // 16]))
 
-        for i, (load, off, w, v) in enumerate(UNITS):
-            a, c0 = LOADS[load][0], LOADS[load][1] + off
+        gw = {}
+
+        def gather_words(a, k, tag, parts=1):
+            gw[a, k] = held.tile([P, W], U32, name=f"gw{a}_{k}", tag=tag, align_bytes=64)
+            gather(gw[a, k], codes[a], k, parts)
+
+        def views(g, r, lo, hi):
+            return g[:, lo:hi, :], r[:, :, lo:hi].rearrange("p j w -> p w j")
+
+        for i, (a, c0, w, v) in enumerate(PIECES):
             g = held.tile([P, w, 4], BF16, name=f"grp{i}", align_bytes=64)
-            src = raw[load][:].rearrange("p j w -> p w j")
             if v < w:
-                nc.scalar.copy(out=g[:, v:w, :], in_=src[:, off + v : off + w, :])
+                nc.scalar.copy(*views(g, raw[i], v, w))
             if v > 0:
-                nc.vector.tensor_copy(out=g[:, 0:v, :], in_=src[:, off : off + v, :])
+                nc.vector.tensor_copy(*views(g, raw[i], 0, v))
             nc.vector.quantize_mx(
                 out=codes[a][:, c0 : c0 + w].bitcast(FP8X4),
                 scales=plane[4 * a : P, c0 : c0 + w],
                 in_=g[:].rearrange("p w j -> p (w j)"),
             )
-        for k, n in enumerate(BLOCKS):
-            gather(sp[k][0][:], plane, C * STARTS[k], C * n)
+            if a < 2 and c0 + w == T:
+                for k in range(BLOCKS if a == 0 else 2):
+                    gather_words(a, k, f"gw{a}_{k}")
+
+        def pick_scales(k):
+            gather(picked[k], plane, k)
             for a in (1, 2):
-                nc.sync.dma_start(out=sp[k][a][0:112, :].bitcast(I32), in_=sp[k][0][4 * a : 112 + 4 * a, :].bitcast(I32))
-        wt.append(held.tile([P, BLOCKS[-1] * PASSES, 2 * N], U8, name="wt_last", tag="plane", align_bytes=64))
-        load_weights(len(BLOCKS) - 1)
-        gw = {}
-        for a, k, s0, n in WORDS:
-            if (a, k) not in gw:
-                gw[a, k] = held.tile(
-                    [P, C * BLOCKS[k]], U32, name=f"gw{a}_{k}", tag=LATE.get((a, k), f"gw{a}_{k}"), align_bytes=64
-                )
-            gather(gw[a, k][:, s0 : s0 + n], codes[a], C * STARTS[k] + s0, n)
+                c0 = (a - 1) * S + k * W
+                nc.sync.dma_start(out=shifted[0:112, c0 : c0 + W].bitcast(I32), in_=picked[k][4 * a : 112 + 4 * a, :].bitcast(I32))
+
+        pick_scales(0)
+        load_weights(1)
+        pick_scales(1)
+        load_weights(2)
+        gather_words(2, 0, "gw2_0")
+        pick_scales(2)
+        gather_words(2, 1, "gw2_1")
+        gather_words(1, 2, "grp6")
+        gather_words(2, 2, "gw2_2", 2)
 
         def multiply(acc, e, h, a):
-            k = block_of[e]
-            i = e - STARTS[k]
+            k, i = divmod(e, G)
+            scale = picked[k][:, C * i : C * i + C] if a == 0 else shifted[:, (a - 1) * S + C * e : (a - 1) * S + C * e + C]
             nc.tensor.matmul_mx(
                 out=acc[:],
                 lhsT=wt[k][:, 3 * i + a, 256 * h : 256 * h + 256].bitcast(FP4X4),
                 lhsT_scale=ws[:, 3 * e + a, 128 * h : 128 * h + 128],
                 rhs=gw[a, k][:, C * i : C * i + C].bitcast(FP8X4),
-                rhs_scale=sp[k][a][:, C * i : C * i + C],
+                rhs_scale=scale,
                 start=(a == 0),
                 stop=(a == PASSES - 1),
             )
 
-        accs = {}
-        for e in range(LEAD):
-            for h in range(2):
-                accs[e, h] = psum.tile([P, C], F32, name="acc")
-        for a in range(2):
-            for e in range(LEAD):
-                for h in range(2):
-                    multiply(accs[e, h], e, h, a)
         ov = out.rearrange("(h p) (m s) -> h p m s", p=P, m=2)
-        bounds = [sum(STORE_CUTS[:i]) for i in range(len(STORE_CUTS) + 1)]
-        for lo, hi in zip(bounds[:-1], bounds[1:]):
-            for e in range(lo, hi):
-                for h in range(2):
-                    if e < LEAD:
-                        acc = accs[e, h]
-                        multiply(acc, e, h, 2)
-                    else:
-                        acc = psum.tile([P, C], F32, name="acc")
-                        for a in range(PASSES):
-                            multiply(acc, e, h, a)
-                    res, sums = ot[:, h, :, e, :], acc[:].rearrange("p (m u) -> p m u", m=2)
-                    if e >= V_EVAC and h == 1:
-                        nc.vector.tensor_scalar(res, sums, bias[:, h, e : e + 1], 0.0, ADD, MAX)
-                    else:
-                        nc.scalar.activation(out=res, in_=sums, func=RELU, bias=bias[:, h, e : e + 1])
-            for h in range(2):
-                nc.sync.dma_start(
-                    out=ov[h, :, :, 64 * lo : 64 * hi], in_=ot[:, h, :, lo:hi, :].rearrange("p m e u -> p m (e u)")
-                )
+        stored = 0
+        for k in range(BLOCKS):
+            sums = [(e, h) for e in range(G * k, G * k + G) for h in range(2)]
+            accs = {}
+            for e, h in sums:
+                accs[e, h] = psum.tile([P, C], F32, name="acc")
+                multiply(accs[e, h], e, h, 0)
+            for e, h in sums:
+                multiply(accs[e, h], e, h, 1)
+            for e, h in sums:
+                multiply(accs[e, h], e, h, 2)
+                res, acc = ot[:, h, :, e, :], accs[e, h][:].rearrange("p (m u) -> p m u", m=2)
+                if e >= VECTOR_FROM and h == 1:
+                    nc.vector.tensor_scalar(res, acc, bias[:, h, e : e + 1], 0.0, ADD, MAX)
+                else:
+                    nc.scalar.activation(out=res, in_=acc, func=RELU, bias=bias[:, h, e : e + 1])
+                if h == 1 and e + 1 in STORE_ENDS:
+                    for hh in range(2):
+                        nc.sync.dma_start(
+                            out=ov[hh, :, :, 64 * stored : 64 * (e + 1)],
+                            in_=ot[:, hh, :, stored : e + 1, :].rearrange("p m e u -> p m (e u)"),
+                        )
+                    stored = e + 1

@@ -16,7 +16,7 @@ FP8X4 = mybir.dt.float8_e4m3fn_x4
 FP4X4 = mybir.dt.float4_e2m1fn_x4
 RELU = mybir.ActivationFunctionType.Relu
 
-PIECES = [(0, 0, 512, 320), (0, 512, 512, 352), (1, 0, 512, 0), (1, 512, 512, 320), (2, 0, 512, 0), (2, 512, 256, 0), (2, 768, 256, 192)]
+PIECES = [(0, 0, 512, 320), (0, 512, 512, 352), (1, 0, 512, 0), (1, 512, 512, 320), (2, 0, 512, 0), (2, 512, 512, 0)]
 G = 4
 BLOCKS = E // G
 W = G * C
@@ -36,15 +36,18 @@ def tile_moe_eps_lin_relu_kernel(tc, xT, w_words, w_scales, b, offs, out):
         bias = held.tile([P, 2, E], F32, name="bias")
         ws = held.tile([P, E * PASSES, N], U8, name="ws", align_bytes=64)
         plane = held.tile([P, T], U8, name="plane", align_bytes=64)
+        plane2 = held.tile([P, T], U8, name="plane2", align_bytes=64)
+        picked01 = held.tile([P, S], U8, name="picked01", align_bytes=64)
         codes = [held.tile([P, T], U32, name=f"codes{a}", align_bytes=64) for a in range(PASSES)]
         ot = held.tile([P, 2, 2, E, 64], F32, name="ot", align_bytes=64)
         picked = [held.tile([P, W], U8, name=f"picked{k}", align_bytes=64) for k in range(BLOCKS)]
-        shifted = held.tile([P, 2 * S], U8, name="shifted", align_bytes=64)
+        shifted = held.tile([P, S], U8, name="shifted", align_bytes=64)
         wt = [held.tile([P, G * PASSES, 2 * N], U8, name=f"wt{k}", align_bytes=64) for k in range(BLOCKS)]
         warm = held.tile([P, 1], F32, name="warm")
         nc.vector.memset(warm[:], 0)
         nc.scalar.activation(out=warm[:], in_=warm[:], func=RELU)
         nc.vector.memset(plane[:].bitcast(I32), 0)
+        nc.vector.memset(plane2[:].bitcast(I32), 0)
         nc.vector.memset(ws[:].rearrange("p g n -> p (g n)").bitcast(I32), 0)
         nc.vector.memset(shifted[:].bitcast(I32), 0)
 
@@ -89,32 +92,34 @@ def tile_moe_eps_lin_relu_kernel(tc, xT, w_words, w_scales, b, offs, out):
                 nc.vector.tensor_copy(*views(g, raw[i], 0, v))
             nc.vector.quantize_mx(
                 out=codes[a][:, c0 : c0 + w].bitcast(FP8X4),
-                scales=plane[4 * a : P, c0 : c0 + w],
+                scales=plane2[:, c0 : c0 + w] if a == 2 else plane[4 * a : P, c0 : c0 + w],
                 in_=g[:].rearrange("p w j -> p (w j)"),
             )
+            if a == 1 and c0 + w == T:
+                for s0 in (0, S // 2):
+                    nc.vector.tensor_copy(picked01[:, s0 : s0 + S // 2], plane[:].indirect(offsets[:, s0 // 16 : (s0 + S // 2) // 16]))
+                nc.sync.dma_start(out=shifted[0:112, :].bitcast(I32), in_=picked01[4:116, :].bitcast(I32))
+                load_weights(1)
+                load_weights(2)
             if a < 2 and c0 + w == T:
-                for k in range(BLOCKS if a == 0 else 2):
+                for k in range(BLOCKS if a == 0 else 1):
                     gather_words(a, k, f"gw{a}_{k}")
 
         def pick_scales(k):
-            gather(picked[k], plane, k)
-            for a in (1, 2):
-                c0 = (a - 1) * S + k * W
-                nc.sync.dma_start(out=shifted[0:112, c0 : c0 + W].bitcast(I32), in_=picked[k][4 * a : 112 + 4 * a, :].bitcast(I32))
+            gather(picked[k], plane2, k)
 
+        gather_words(1, 1, "grp4")
         pick_scales(0)
-        load_weights(1)
-        pick_scales(1)
-        load_weights(2)
         gather_words(2, 0, "gw2_0")
-        pick_scales(2)
+        pick_scales(1)
         gather_words(2, 1, "gw2_1")
-        gather_words(1, 2, "grp6")
+        gather_words(1, 2, "grp5")
+        pick_scales(2)
         gather_words(2, 2, "gw2_2", 2)
 
         def multiply(acc, e, h, a):
             k, i = divmod(e, G)
-            scale = picked[k][:, C * i : C * i + C] if a == 0 else shifted[:, (a - 1) * S + C * e : (a - 1) * S + C * e + C]
+            scale = picked[k][:, C * i : C * i + C] if a == 2 else (picked01, shifted)[a][:, C * e : C * e + C]
             nc.tensor.matmul_mx(
                 out=acc[:],
                 lhsT=wt[k][:, 3 * i + a, 256 * h : 256 * h + 256].bitcast(FP4X4),

@@ -82,7 +82,10 @@ def tile_moe_eps_lin_relu_kernel(tc, xT, w_words, w_scales, b, offs, out):
             gather(gw[a, k], codes[a], k, parts)
 
         def views(g, r, lo, hi):
-            return g[:, lo:hi, :], r[:, :, lo:hi].rearrange("p j w -> p w j")
+            return (
+                g[:, lo:hi, :].rearrange("p (c i) j -> p c j i", i=2),
+                r[:, :, lo:hi].rearrange("p j (c i) -> p c j i", i=2),
+            )
 
         for i, (a, c0, w, v) in enumerate(PIECES):
             g = held.tile([P, w, 4], BF16, name=f"grp{i}", align_bytes=64)

@@ -42,7 +42,7 @@ def tile_moe_eps_lin_relu_kernel(tc, xT, w_words, w_scales, b, offs, out):
         ot = held.tile([P, 2, 2, E, 64], F32, name="ot", align_bytes=64)
         picked = [held.tile([P, W], U8, name=f"picked{k}", align_bytes=64) for k in range(BLOCKS)]
         shifted = held.tile([P, S], U8, name="shifted", align_bytes=64)
-        wt = [held.tile([P, G * PASSES, 2 * N], U8, name=f"wt{k}", align_bytes=64) for k in range(BLOCKS)]
+        wt = [[held.tile([P, 2 * N], U8, name=f"wt{e}_{a}", align_bytes=64) for a in range(PASSES)] for e in range(E)]
         warm = held.tile([P, 1], F32, name="warm")
         nc.vector.memset(warm[:], 0)
         nc.scalar.activation(out=warm[:], in_=warm[:], func=RELU)
@@ -58,15 +58,16 @@ def tile_moe_eps_lin_relu_kernel(tc, xT, w_words, w_scales, b, offs, out):
             raw.append(r)
             if i == 0:
                 nc.sync.dma_start(offsets[:], offs)
-        ww = w_words.bitcast(I32).rearrange("e a p n -> p (e a) n")
+        ww = w_words.bitcast(I32)
         wsc = w_scales.bitcast(I32).rearrange("e a q n -> q (e a) n")
         for r in range(4):
             nc.sync.dma_start(out=ws[r:P:32, :, :].bitcast(I32), in_=wsc[r:16:4])
 
         def load_weights(k):
-            nc.sync.dma_start(out=wt[k][:].bitcast(I32), in_=ww[:, G * PASSES * k : G * PASSES * (k + 1), :])
+            for a in range(PASSES):
+                for e in range(G * k, G * k + G):
+                    nc.sync.dma_start(out=wt[e][a][:].bitcast(I32), in_=ww[e, a])
 
-        load_weights(0)
         nc.sync.dma_start(out=bias[:], in_=b.rearrange("(h p) e -> p h e", p=P))
 
         def gather(dst, window, k, parts=1):
@@ -102,8 +103,8 @@ def tile_moe_eps_lin_relu_kernel(tc, xT, w_words, w_scales, b, offs, out):
                 for s0 in (0, S // 2):
                     nc.vector.tensor_copy(picked01[:, s0 : s0 + S // 2], plane[:].indirect(offsets[:, s0 // 16 : (s0 + S // 2) // 16]))
                 nc.sync.dma_start(out=shifted[0:112, :].bitcast(I32), in_=picked01[4:116, :].bitcast(I32))
-                load_weights(1)
-                load_weights(2)
+                for k in range(BLOCKS):
+                    load_weights(k)
             if a < 2 and c0 + w == T:
                 for k in range(BLOCKS if a == 0 else 1):
                     gather_words(a, k, f"gw{a}_{k}")
@@ -125,7 +126,7 @@ def tile_moe_eps_lin_relu_kernel(tc, xT, w_words, w_scales, b, offs, out):
             scale = picked[k][:, C * i : C * i + C] if a == 2 else (picked01, shifted)[a][:, C * e : C * e + C]
             nc.tensor.matmul_mx(
                 out=acc[:],
-                lhsT=wt[k][:, 3 * i + a, 256 * h : 256 * h + 256].bitcast(FP4X4),
+                lhsT=wt[e][a][:, 256 * h : 256 * h + 256].bitcast(FP4X4),
                 lhsT_scale=ws[:, 3 * e + a, 128 * h : 128 * h + 128],
                 rhs=gw[a, k][:, C * i : C * i + C].bitcast(FP8X4),
                 rhs_scale=scale,

@@ -15,15 +15,17 @@ U8 = mybir.dt.uint8
 FP8X4 = mybir.dt.float8_e4m3fn_x4
 FP4X4 = mybir.dt.float4_e2m1fn_x4
 RELU = mybir.ActivationFunctionType.Relu
+ADD = mybir.AluOpType.add
+MAX = mybir.AluOpType.max
 
-PIECES = [(0, 0, 512, 320), (0, 512, 512, 352), (1, 0, 512, 0), (1, 512, 512, 320), (2, 0, 512, 0), (2, 512, 512, 0)]
+LOADS = ((0, 0, 512), (0, 512, 1024), (1, 0, 512), (1, 512, 1024), (2, 0, 1024))
+STRETCHES = ((0, 0, 512, 320), (0, 512, 1024, 352), (1, 0, 512, 0), (1, 512, 1024, 320), (2, 0, 512, 0), (2, 512, 1024, 0))
 G = 4
 BLOCKS = E // G
 W = G * C
-STORE_ENDS = (4, 8, 10, 12)
-VECTOR_FROM = 10
-ADD = mybir.AluOpType.add
-MAX = mybir.AluOpType.max
+LAST_PASS_ENDS = (4, 8, 10, 12)
+SHIFT_ROWS = 112
+AHEAD_OF_SHIFT = 8
 
 
 def tile_moe_eps_lin_relu_kernel(tc, xT, w_words, w_scales, b, offs, out):
@@ -35,126 +37,123 @@ def tile_moe_eps_lin_relu_kernel(tc, xT, w_words, w_scales, b, offs, out):
         offsets = held.tile([P, S // 16], U16, name="offsets")
         bias = held.tile([P, 2, E], F32, name="bias")
         ws = held.tile([P, E * PASSES, N], U8, name="ws", align_bytes=64)
-        plane = held.tile([P, T], U8, name="plane", align_bytes=64)
-        plane2 = held.tile([P, T], U8, name="plane2", align_bytes=64)
+        planes = held.tile([P, 2 * T], U8, name="planes", align_bytes=64)
         picked01 = held.tile([P, S], U8, name="picked01", align_bytes=64)
-        codes = [held.tile([P, T], U32, name=f"codes{a}", align_bytes=64) for a in range(PASSES)]
+        moved = held.tile([P, S], U8, name="moved", align_bytes=64)
+        picked2 = held.tile([P, S], U8, name="picked2", align_bytes=64)
+        codes = held.tile([P, (PASSES + 1) * T], U32, name="codes", align_bytes=64)
+        slots = [held.tile([P, S], U32, name=f"slots{a}", align_bytes=64) for a in range(PASSES)]
         ot = held.tile([P, 2, 2, E, 64], F32, name="ot", align_bytes=64)
-        picked = [held.tile([P, W], U8, name=f"picked{k}", align_bytes=64) for k in range(BLOCKS)]
-        shifted = held.tile([P, S], U8, name="shifted", align_bytes=64)
         wt = [[held.tile([P, 2 * N], U8, name=f"wt{e}_{a}", align_bytes=64) for a in range(PASSES)] for e in range(E)]
-        warm = held.tile([P, 1], F32, name="warm")
-        nc.vector.memset(warm[:], 0)
-        nc.scalar.activation(out=warm[:], in_=warm[:], func=RELU)
-        nc.vector.memset(plane[:].bitcast(I32), 0)
-        nc.vector.memset(plane2[:].bitcast(I32), 0)
+        nc.vector.memset(planes[:].bitcast(I32), 0)
         nc.vector.memset(ws[:].rearrange("p g n -> p (g n)").bitcast(I32), 0)
-        nc.vector.memset(shifted[:].bitcast(I32), 0)
+        nc.vector.memset(moved[:].bitcast(I32), 0)
+        nc.vector.memset(codes[:, PASSES * T :].bitcast(I32), 0)
 
         raw = []
-        for i, (a, c0, w, v) in enumerate(PIECES):
-            r = held.tile([P, 4, w], F32, name=f"raw{i}", align_bytes=64)
-            nc.sync.dma_start(out=r[:], in_=xT[512 * a : 512 * a + 512, c0 : c0 + w].rearrange("(p j) w -> p j w", j=4))
-            raw.append(r)
-            if i == 0:
+        for i, (a, c0, c1) in enumerate(LOADS):
+            x = held.tile([P, 4, c1 - c0], F32, name=f"raw{i}", align_bytes=64)
+            nc.sync.dma_start(out=x[:], in_=xT[512 * a : 512 * a + 512, c0:c1].rearrange("(p j) w -> p j w", j=4))
+            raw.append(x)
+            if i == 1:
                 nc.sync.dma_start(offsets[:], offs)
-        ww = w_words.bitcast(I32)
         wsc = w_scales.bitcast(I32).rearrange("e a q n -> q (e a) n")
         for r in range(4):
             nc.sync.dma_start(out=ws[r:P:32, :, :].bitcast(I32), in_=wsc[r:16:4])
-
-        def load_weights(k):
-            for a in range(PASSES):
-                for e in range(G * k, G * k + G):
-                    nc.sync.dma_start(out=wt[e][a][:].bitcast(I32), in_=ww[e, a])
-
         nc.sync.dma_start(out=bias[:], in_=b.rearrange("(h p) e -> p h e", p=P))
 
-        def gather(dst, window, k, parts=1):
-            n = W // parts
-            for s0 in range(0, W, n):
-                lo = (k * W + s0) // 16
-                nc.vector.tensor_copy(dst[:, s0 : s0 + n], window[:].indirect(offsets[:, lo : lo + n // 16]))
+        ww = w_words.bitcast(I32)
+        order = [(e, a) for k in range(BLOCKS) for a in range(PASSES) for e in range(G * k, G * k + G)]
 
-        gw = {}
+        def load_weights(steps):
+            for e, a in steps:
+                nc.sync.dma_start(out=wt[e][a][:].bitcast(I32), in_=ww[e, a])
 
-        def gather_words(a, k, tag, parts=1):
-            gw[a, k] = held.tile([P, W], U32, name=f"gw{a}_{k}", tag=tag, align_bytes=64)
-            gather(gw[a, k], codes[a], k, parts)
+        load_weights(order[:AHEAD_OF_SHIFT])
 
-        def views(g, r, lo, hi):
-            return (
-                g[:, lo:hi, :].rearrange("p (c i) j -> p c j i", i=2),
-                r[:, :, lo:hi].rearrange("p j (c i) -> p c j i", i=2),
-            )
+        def gather(dst, window, s0, s1):
+            nc.vector.tensor_copy(dst[:, s0:s1], window.indirect(offsets[:, s0 // 16 : s1 // 16]))
 
-        for i, (a, c0, w, v) in enumerate(PIECES):
-            g = held.tile([P, w, 4], BF16, name=f"grp{i}", align_bytes=64)
-            if v < w:
-                nc.scalar.copy(*views(g, raw[i], v, w))
+        def interleave(k):
+            a, t0, t1, v = STRETCHES[k]
+            g = held.tile([P, t1 - t0, 4], BF16, name=f"grouped{k}", align_bytes=64)
+            x, c0 = [(raw[i], c0) for i, (pa, c0, c1) in enumerate(LOADS) if pa == a and c0 <= t0 < c1][0]
+
+            def views(lo, hi):
+                return (
+                    g[:, lo:hi, :].rearrange("p (c i) j -> p c j i", i=2),
+                    x[:, :, t0 - c0 + lo : t0 - c0 + hi].rearrange("p j (c i) -> p c j i", i=2),
+                )
+
+            nc.scalar.copy(*views(v, t1 - t0))
             if v > 0:
-                nc.vector.tensor_copy(*views(g, raw[i], 0, v))
+                nc.vector.tensor_copy(*views(0, v))
+            return g
+
+        def first_word(a):
+            return (PASSES - 1 - a) * T
+
+        def quantize(k, g):
+            a, t0, t1, v = STRETCHES[k]
             nc.vector.quantize_mx(
-                out=codes[a][:, c0 : c0 + w].bitcast(FP8X4),
-                scales=plane2[:, c0 : c0 + w] if a == 2 else plane[4 * a : P, c0 : c0 + w],
+                out=codes[:, first_word(a) + t0 : first_word(a) + t1].bitcast(FP8X4),
+                scales=planes[:, T + t0 : T + t1] if a == 2 else planes[4 * a : P, t0:t1],
                 in_=g[:].rearrange("p w j -> p (w j)"),
             )
-            if a == 1 and c0 + w == T:
-                for s0 in (0, S // 2):
-                    nc.vector.tensor_copy(picked01[:, s0 : s0 + S // 2], plane[:].indirect(offsets[:, s0 // 16 : (s0 + S // 2) // 16]))
-                nc.sync.dma_start(out=shifted[0:112, :].bitcast(I32), in_=picked01[4:116, :].bitcast(I32))
-                for k in range(BLOCKS):
-                    load_weights(k)
-            if a < 2 and c0 + w == T:
-                for k in range(BLOCKS if a == 0 else 1):
-                    gather_words(a, k, f"gw{a}_{k}")
 
-        def pick_scales(k):
-            gather(picked[k], plane2, k)
+        for a in range(PASSES):
+            mine = [k for k in range(len(STRETCHES)) if STRETCHES[k][0] == a]
+            grouped = [interleave(k) for k in mine]
+            for k, g in zip(mine, grouped):
+                quantize(k, g)
+            if a == 1:
+                gather(picked01, planes[:], 0, S)
+                nc.sync.dma_start(out=moved[0:SHIFT_ROWS, :].bitcast(I32), in_=picked01[4 : 4 + SHIFT_ROWS, :].bitcast(I32))
+                load_weights(order[AHEAD_OF_SHIFT:])
+            if a < 2:
+                gather(slots[a], codes[:, first_word(a) : first_word(a) + 2 * T], 0, S)
 
-        gather_words(1, 1, "grp4")
-        pick_scales(0)
-        gather_words(2, 0, "gw2_0")
-        pick_scales(1)
-        gather_words(2, 1, "gw2_1")
-        gather_words(1, 2, "grp5")
-        pick_scales(2)
-        gather_words(2, 2, "gw2_2", 2)
+        e0 = 0
+        for e1 in LAST_PASS_ENDS:
+            if e0 % G == 0:
+                gather(picked2, planes[:, T:], C * e0, C * e0 + W)
+            gather(slots[2], codes[:, 0:T], C * e0, C * e1)
+            e0 = e1
 
-        def multiply(acc, e, h, a):
-            k, i = divmod(e, G)
-            scale = picked[k][:, C * i : C * i + C] if a == 2 else (picked01, shifted)[a][:, C * e : C * e + C]
-            nc.tensor.matmul_mx(
-                out=acc[:],
-                lhsT=wt[e][a][:, 256 * h : 256 * h + 256].bitcast(FP4X4),
-                lhsT_scale=ws[:, 3 * e + a, 128 * h : 128 * h + 128],
-                rhs=gw[a, k][:, C * i : C * i + C].bitcast(FP8X4),
-                rhs_scale=scale,
-                start=(a == 0),
-                stop=(a == PASSES - 1),
-            )
+        acc = {}
+
+        def multiply(e, a):
+            if a == 0:
+                acc[e] = psum.tile([P, 2, C], F32, name="acc")
+            for h in range(2):
+                nc.tensor.matmul_mx(
+                    out=acc[e][:, h, :],
+                    lhsT=wt[e][a][:, 256 * h : 256 * h + 256].bitcast(FP4X4),
+                    lhsT_scale=ws[:, 3 * e + a, 128 * h : 128 * h + 128],
+                    rhs=slots[a][:, C * e : C * e + C].bitcast(FP8X4),
+                    rhs_scale=(picked01, moved, picked2)[a][:, C * e : C * e + C],
+                    start=(a == 0 and h == 0),
+                    stop=(a == PASSES - 1 and h == 1),
+                )
+
+        def finish(e):
+            for h in range(2):
+                res, sums = ot[:, h, :, e, :], acc[e][:, h, :].rearrange("p (m u) -> p m u", m=2)
+                if e == E - 1:
+                    nc.vector.tensor_scalar(res, sums, bias[:, h, e : e + 1], 0.0, ADD, MAX)
+                else:
+                    nc.scalar.activation(out=res, in_=sums, func=RELU, bias=bias[:, h, e : e + 1])
 
         ov = out.rearrange("(h p) (m s) -> h p m s", p=P, m=2)
         stored = 0
-        for k in range(BLOCKS):
-            sums = [(e, h) for e in range(G * k, G * k + G) for h in range(2)]
-            accs = {}
-            for e, h in sums:
-                accs[e, h] = psum.tile([P, C], F32, name="acc")
-                multiply(accs[e, h], e, h, 0)
-            for e, h in sums:
-                multiply(accs[e, h], e, h, 1)
-            for e, h in sums:
-                multiply(accs[e, h], e, h, 2)
-                res, acc = ot[:, h, :, e, :], accs[e, h][:].rearrange("p (m u) -> p m u", m=2)
-                if e >= VECTOR_FROM and h == 1:
-                    nc.vector.tensor_scalar(res, acc, bias[:, h, e : e + 1], 0.0, ADD, MAX)
-                else:
-                    nc.scalar.activation(out=res, in_=acc, func=RELU, bias=bias[:, h, e : e + 1])
-                if h == 1 and e + 1 in STORE_ENDS:
-                    for hh in range(2):
+        for e, a in order:
+            multiply(e, a)
+            if a == PASSES - 1:
+                finish(e)
+                if e + 1 in LAST_PASS_ENDS:
+                    for h in range(2):
                         nc.sync.dma_start(
-                            out=ov[hh, :, :, 64 * stored : 64 * (e + 1)],
-                            in_=ot[:, hh, :, stored : e + 1, :].rearrange("p m e u -> p m (e u)"),
+                            out=ov[h, :, :, 64 * stored : 64 * (e + 1)],
+                            in_=ot[:, h, :, stored : e + 1, :].rearrange("p m e u -> p m (e u)"),
                         )
                     stored = e + 1

@@ -2,10 +2,11 @@ import concourse.mybir as mybir
 
 FLOPS = 2 * 1536 * 1536 * 256
 
-K, T, E, C, N = 1536, 1024, 12, 128, 256
+T, E, C, N = 1024, 12, 128, 256
 P = 128
 PASSES = 3
 S = E * C
+RANKS = 2
 F32 = mybir.dt.float32
 BF16 = mybir.dt.bfloat16
 I32 = mybir.dt.int32
@@ -19,13 +20,12 @@ ADD = mybir.AluOpType.add
 MAX = mybir.AluOpType.max
 
 LOADS = ((0, 0, 512), (0, 512, 1024), (1, 0, 512), (1, 512, 1024), (2, 0, 1024))
-STRETCHES = ((0, 0, 512, 320), (0, 512, 1024, 352), (1, 0, 512, 0), (1, 512, 1024, 320), (2, 0, 512, 0), (2, 512, 1024, 0))
+STRETCHES = ((0, 0, 512, 320), (0, 512, 1024, 352), (1, 0, 512, 0), (1, 512, 1024, 320), (2, 0, 512, 0), (2, 512, 1024, 64))
 G = 4
 BLOCKS = E // G
-W = G * C
 LAST_PASS_ENDS = (4, 8, 10, 12)
 SHIFT_ROWS = 112
-AHEAD_OF_SHIFT = 8
+AHEAD_OF_SHIFT = 7
 
 
 def tile_moe_eps_lin_relu_kernel(tc, xT, w_words, w_scales, b, offs, out):
@@ -36,115 +36,118 @@ def tile_moe_eps_lin_relu_kernel(tc, xT, w_words, w_scales, b, offs, out):
     ):
         offsets = held.tile([P, S // 16], U16, name="offsets")
         bias = held.tile([P, 2, E], F32, name="bias")
-        ws = held.tile([P, E * PASSES, N], U8, name="ws", align_bytes=64)
-        planes = held.tile([P, 2 * T], U8, name="planes", align_bytes=64)
+        w_scale = held.tile([P, E * PASSES, N], U8, name="ws", align_bytes=64)
+        token_scale = held.tile([P, 2 * T], U8, name="planes", align_bytes=64)
         picked01 = held.tile([P, S], U8, name="picked01", align_bytes=64)
-        moved = held.tile([P, S], U8, name="moved", align_bytes=64)
+        moved1 = held.tile([P, S], U8, name="moved", align_bytes=64)
         picked2 = held.tile([P, S], U8, name="picked2", align_bytes=64)
-        codes = held.tile([P, (PASSES + 1) * T], U32, name="codes", align_bytes=64)
-        slots = [held.tile([P, S], U32, name=f"slots{a}", align_bytes=64) for a in range(PASSES)]
-        ot = held.tile([P, 2, 2, E, 64], F32, name="ot", align_bytes=64)
-        wt = [[held.tile([P, 2 * N], U8, name=f"wt{e}_{a}", align_bytes=64) for a in range(PASSES)] for e in range(E)]
-        nc.vector.memset(planes[:].bitcast(I32), 0)
-        nc.vector.memset(ws[:].rearrange("p g n -> p (g n)").bitcast(I32), 0)
-        nc.vector.memset(moved[:].bitcast(I32), 0)
-        nc.vector.memset(codes[:, PASSES * T :].bitcast(I32), 0)
+        token_words = held.tile([P, (PASSES + 1) * T], U32, name="codes", align_bytes=64)
+        slot_words = [held.tile([P, S], U32, name=f"slots{a}", align_bytes=64) for a in range(PASSES)]
+        results = held.tile([P, 2, RANKS, E, C // RANKS], F32, name="ot", align_bytes=64)
+        weights = [[held.tile([P, 2 * N], U8, name=f"wt{e}_{a}", align_bytes=64) for a in range(PASSES)] for e in range(E)]
+        nc.vector.memset(token_scale[:].bitcast(I32), 0)
+        nc.vector.memset(w_scale[:].rearrange("p g n -> p (g n)").bitcast(I32), 0)
+        nc.vector.memset(moved1[:].bitcast(I32), 0)
+        nc.vector.memset(token_words[:, PASSES * T :].bitcast(I32), 0)
 
         raw = []
         for i, (a, c0, c1) in enumerate(LOADS):
             x = held.tile([P, 4, c1 - c0], F32, name=f"raw{i}", align_bytes=64)
             nc.sync.dma_start(out=x[:], in_=xT[512 * a : 512 * a + 512, c0:c1].rearrange("(p j) w -> p j w", j=4))
             raw.append(x)
-            if i == 1:
+            if c1 == T and a == 0:
                 nc.sync.dma_start(offsets[:], offs)
-        wsc = w_scales.bitcast(I32).rearrange("e a q n -> q (e a) n")
-        for r in range(4):
-            nc.sync.dma_start(out=ws[r:P:32, :, :].bitcast(I32), in_=wsc[r:16:4])
+
+        scale_rows = w_scales.bitcast(I32).rearrange("e a q n -> q (e a) n")
+        for k in range(BLOCKS):
+            rows = slice(G * PASSES * k, G * PASSES * (k + 1))
+            for r in range(4):
+                nc.sync.dma_start(out=w_scale[r:P:32, rows, :].bitcast(I32), in_=scale_rows[r:16:4, rows, :])
         nc.sync.dma_start(out=bias[:], in_=b.rearrange("(h p) e -> p h e", p=P))
 
-        ww = w_words.bitcast(I32)
+        weight_words = w_words.bitcast(I32)
         order = [(e, a) for k in range(BLOCKS) for a in range(PASSES) for e in range(G * k, G * k + G)]
 
         def load_weights(steps):
             for e, a in steps:
-                nc.sync.dma_start(out=wt[e][a][:].bitcast(I32), in_=ww[e, a])
+                nc.sync.dma_start(out=weights[e][a][:].bitcast(I32), in_=weight_words[e, a])
 
         load_weights(order[:AHEAD_OF_SHIFT])
 
         def gather(dst, window, s0, s1):
             nc.vector.tensor_copy(dst[:, s0:s1], window.indirect(offsets[:, s0 // 16 : s1 // 16]))
 
-        def interleave(k):
-            a, t0, t1, v = STRETCHES[k]
-            g = held.tile([P, t1 - t0, 4], BF16, name=f"grouped{k}", align_bytes=64)
-            x, c0 = [(raw[i], c0) for i, (pa, c0, c1) in enumerate(LOADS) if pa == a and c0 <= t0 < c1][0]
+        def interleave(stretch):
+            a, t0, t1, on_vector = STRETCHES[stretch]
+            grouped = held.tile([P, t1 - t0, 4], BF16, name=f"grouped{stretch}", align_bytes=64)
+            x, c0 = [(raw[i], lo) for i, (pa, lo, hi) in enumerate(LOADS) if pa == a and lo <= t0 < hi][0]
 
             def views(lo, hi):
                 return (
-                    g[:, lo:hi, :].rearrange("p (c i) j -> p c j i", i=2),
+                    grouped[:, lo:hi, :].rearrange("p (c i) j -> p c j i", i=2),
                     x[:, :, t0 - c0 + lo : t0 - c0 + hi].rearrange("p j (c i) -> p c j i", i=2),
                 )
 
-            nc.scalar.copy(*views(v, t1 - t0))
-            if v > 0:
-                nc.vector.tensor_copy(*views(0, v))
-            return g
+            nc.scalar.copy(*views(on_vector, t1 - t0))
+            if on_vector > 0:
+                nc.vector.tensor_copy(*views(0, on_vector))
+            return grouped
 
         def first_word(a):
             return (PASSES - 1 - a) * T
 
-        def quantize(k, g):
-            a, t0, t1, v = STRETCHES[k]
+        def quantize(stretch, grouped):
+            a, t0, t1 = STRETCHES[stretch][:3]
             nc.vector.quantize_mx(
-                out=codes[:, first_word(a) + t0 : first_word(a) + t1].bitcast(FP8X4),
-                scales=planes[:, T + t0 : T + t1] if a == 2 else planes[4 * a : P, t0:t1],
-                in_=g[:].rearrange("p w j -> p (w j)"),
+                out=token_words[:, first_word(a) + t0 : first_word(a) + t1].bitcast(FP8X4),
+                scales=token_scale[:, T + t0 : T + t1] if a == 2 else token_scale[4 * a : P, t0:t1],
+                in_=grouped[:].rearrange("p w j -> p (w j)"),
             )
 
         for a in range(PASSES):
-            mine = [k for k in range(len(STRETCHES)) if STRETCHES[k][0] == a]
-            grouped = [interleave(k) for k in mine]
-            for k, g in zip(mine, grouped):
-                quantize(k, g)
+            stretches = [i for i in range(len(STRETCHES)) if STRETCHES[i][0] == a]
+            for stretch, grouped in zip(stretches, [interleave(i) for i in stretches]):
+                quantize(stretch, grouped)
             if a == 1:
-                gather(picked01, planes[:], 0, S)
-                nc.sync.dma_start(out=moved[0:SHIFT_ROWS, :].bitcast(I32), in_=picked01[4 : 4 + SHIFT_ROWS, :].bitcast(I32))
+                gather(picked01, token_scale[:], 0, S)
+                nc.sync.dma_start(out=moved1[0:SHIFT_ROWS, :].bitcast(I32), in_=picked01[4 : 4 + SHIFT_ROWS, :].bitcast(I32))
                 load_weights(order[AHEAD_OF_SHIFT:])
             if a < 2:
-                gather(slots[a], codes[:, first_word(a) : first_word(a) + 2 * T], 0, S)
+                gather(slot_words[a], token_words[:, first_word(a) : first_word(a) + 2 * T], 0, S)
 
         e0 = 0
         for e1 in LAST_PASS_ENDS:
             if e0 % G == 0:
-                gather(picked2, planes[:, T:], C * e0, C * e0 + W)
-            gather(slots[2], codes[:, 0:T], C * e0, C * e1)
+                gather(picked2, token_scale[:, T:], C * e0, C * (e0 + G))
+            gather(slot_words[2], token_words[:, 0:T], C * e0, C * e1)
             e0 = e1
 
-        acc = {}
+        sums = {}
 
         def multiply(e, a):
             if a == 0:
-                acc[e] = psum.tile([P, 2, C], F32, name="acc")
+                sums[e] = psum.tile([P, 2, C], F32, name="acc")
             for h in range(2):
                 nc.tensor.matmul_mx(
-                    out=acc[e][:, h, :],
-                    lhsT=wt[e][a][:, 256 * h : 256 * h + 256].bitcast(FP4X4),
-                    lhsT_scale=ws[:, 3 * e + a, 128 * h : 128 * h + 128],
-                    rhs=slots[a][:, C * e : C * e + C].bitcast(FP8X4),
-                    rhs_scale=(picked01, moved, picked2)[a][:, C * e : C * e + C],
+                    out=sums[e][:, h, :],
+                    lhsT=weights[e][a][:, 2 * P * h : 2 * P * (h + 1)].bitcast(FP4X4),
+                    lhsT_scale=w_scale[:, PASSES * e + a, P * h : P * (h + 1)],
+                    rhs=slot_words[a][:, C * e : C * e + C].bitcast(FP8X4),
+                    rhs_scale=(picked01, moved1, picked2)[a][:, C * e : C * e + C],
                     start=(a == 0 and h == 0),
                     stop=(a == PASSES - 1 and h == 1),
                 )
 
         def finish(e):
             for h in range(2):
-                res, sums = ot[:, h, :, e, :], acc[e][:, h, :].rearrange("p (m u) -> p m u", m=2)
+                res, acc = results[:, h, :, e, :], sums[e][:, h, :].rearrange("p (m u) -> p m u", m=RANKS)
                 if e == E - 1:
-                    nc.vector.tensor_scalar(res, sums, bias[:, h, e : e + 1], 0.0, ADD, MAX)
+                    nc.vector.tensor_scalar(res, acc, bias[:, h, e : e + 1], 0.0, ADD, MAX)
                 else:
-                    nc.scalar.activation(out=res, in_=sums, func=RELU, bias=bias[:, h, e : e + 1])
+                    nc.scalar.activation(out=res, in_=acc, func=RELU, bias=bias[:, h, e : e + 1])
 
-        ov = out.rearrange("(h p) (m s) -> h p m s", p=P, m=2)
+        out_rows = out.rearrange("(h p) (m s) -> h p m s", p=P, m=RANKS)
+        places = C // RANKS
         stored = 0
         for e, a in order:
             multiply(e, a)
@@ -153,7 +156,7 @@ def tile_moe_eps_lin_relu_kernel(tc, xT, w_words, w_scales, b, offs, out):
                 if e + 1 in LAST_PASS_ENDS:
                     for h in range(2):
                         nc.sync.dma_start(
-                            out=ov[h, :, :, 64 * stored : 64 * (e + 1)],
-                            in_=ot[:, h, :, stored : e + 1, :].rearrange("p m e u -> p m (e u)"),
+                            out=out_rows[h, :, :, places * stored : places * (e + 1)],
+                            in_=results[:, h, :, stored : e + 1, :].rearrange("p m e u -> p m (e u)"),
                         )
                     stored = e + 1

@@ -19,39 +19,43 @@ RELU = mybir.ActivationFunctionType.Relu
 ADD = mybir.AluOpType.add
 MAX = mybir.AluOpType.max
 
-LOADS = ((0, 0, 512), (0, 512, 1024), (1, 0, 512), (1, 512, 1024), (2, 0, 1024))
-STRETCHES = ((0, 0, 512, 320), (0, 512, 1024, 352), (1, 0, 512, 0), (1, 512, 1024, 320), (2, 0, 512, 0), (2, 512, 1024, 64))
+LOADS = (
+    (0, 0, 512, 320), (0, 512, 768, 0), (0, 768, 1024, 176),
+    (1, 0, 256, 0), (1, 256, 512, 0), (1, 512, 768, 0), (1, 768, 1024, 160),
+    (2, 0, 512, 0), (2, 512, 1024, 0),
+)
+STRETCHES = ((0, 0, 512), (0, 512, 768), (0, 768, 1024), (1, 0, 512), (1, 512, 768), (1, 768, 1024), (2, 0, 512), (2, 512, 1024))
 G = 4
 BLOCKS = E // G
 LAST_PASS_ENDS = (4, 8, 10, 12)
 SHIFT_ROWS = 112
-AHEAD_OF_SHIFT = 7
+AHEAD_OF_SHIFT = 2
 
 
 def tile_moe_eps_lin_relu_kernel(tc, xT, w_words, w_scales, b, offs, out):
     nc = tc.nc
     with (
         tc.tile_pool(name="held", bufs=1) as held,
-        tc.psum_pool(name="psum", bufs=8) as psum,
+        tc.psum_pool(name="psum", bufs=1) as psum,
     ):
         offsets = held.tile([P, S // 16], U16, name="offsets")
-        bias = held.tile([P, 2, E], F32, name="bias")
+        bias = held.tile([P, 2, 16], F32, name="bias", align_bytes=64)
         w_scale = held.tile([P, E * PASSES, N], U8, name="ws", align_bytes=64)
         token_scale = held.tile([P, 2 * T], U8, name="planes", align_bytes=64)
         picked01 = held.tile([P, S], U8, name="picked01", align_bytes=64)
         moved1 = held.tile([P, S], U8, name="moved", align_bytes=64)
         picked2 = held.tile([P, S], U8, name="picked2", align_bytes=64)
-        token_words = held.tile([P, (PASSES + 1) * T], U32, name="codes", align_bytes=64)
+        token_words = held.tile([P, PASSES * T], U32, name="codes", align_bytes=64)
         slot_words = [held.tile([P, S], U32, name=f"slots{a}", align_bytes=64) for a in range(PASSES)]
         results = held.tile([P, 2, RANKS, E, C // RANKS], F32, name="ot", align_bytes=64)
-        weights = [[held.tile([P, 2 * N], U8, name=f"wt{e}_{a}", align_bytes=64) for a in range(PASSES)] for e in range(E)]
+        early = [held.tile([P, 2, 2 * N], U8, name=f"early{e}", align_bytes=64) for e in range(E)]
+        late = [held.tile([P, G, 2 * N], U8, name=f"late{k}", align_bytes=64) for k in range(BLOCKS)]
         nc.vector.memset(token_scale[:].bitcast(I32), 0)
         nc.vector.memset(w_scale[:].rearrange("p g n -> p (g n)").bitcast(I32), 0)
         nc.vector.memset(moved1[:].bitcast(I32), 0)
-        nc.vector.memset(token_words[:, PASSES * T :].bitcast(I32), 0)
 
         raw = []
-        for i, (a, c0, c1) in enumerate(LOADS):
+        for i, (a, c0, c1, on_vector) in enumerate(LOADS):
             x = held.tile([P, 4, c1 - c0], F32, name=f"raw{i}", align_bytes=64)
             nc.sync.dma_start(out=x[:], in_=xT[512 * a : 512 * a + 512, c0:c1].rearrange("(p j) w -> p j w", j=4))
             raw.append(x)
@@ -63,57 +67,70 @@ def tile_moe_eps_lin_relu_kernel(tc, xT, w_words, w_scales, b, offs, out):
             rows = slice(G * PASSES * k, G * PASSES * (k + 1))
             for r in range(4):
                 nc.sync.dma_start(out=w_scale[r:P:32, rows, :].bitcast(I32), in_=scale_rows[r:16:4, rows, :])
-        nc.sync.dma_start(out=bias[:], in_=b.rearrange("(h p) e -> p h e", p=P))
 
         weight_words = w_words.bitcast(I32)
-        order = [(e, a) for k in range(BLOCKS) for a in range(PASSES) for e in range(G * k, G * k + G)]
+        steps = [(0, False), (1, False), (0, True), (2, False), (1, True), (2, True)]
+        weight_loads = []
+        for k, last in steps:
+            if last:
+                weight_loads.append((late[k], weight_words[G * k : G * k + G, 2].rearrange("e p n -> p e n")))
+            else:
+                weight_loads.extend((early[e], weight_words[e, 0:2].rearrange("a p n -> p a n")) for e in range(G * k, G * k + G))
 
-        def load_weights(steps):
-            for e, a in steps:
-                nc.sync.dma_start(out=weights[e][a][:].bitcast(I32), in_=weight_words[e, a])
+        def load_weights(loads):
+            for tile, words in loads:
+                nc.sync.dma_start(out=tile[:].bitcast(I32), in_=words)
 
-        load_weights(order[:AHEAD_OF_SHIFT])
+        load_weights(weight_loads[:AHEAD_OF_SHIFT])
 
         def gather(dst, window, s0, s1):
             nc.vector.tensor_copy(dst[:, s0:s1], window.indirect(offsets[:, s0 // 16 : s1 // 16]))
 
-        def interleave(stretch):
-            a, t0, t1, on_vector = STRETCHES[stretch]
-            grouped = held.tile([P, t1 - t0, 4], BF16, name=f"grouped{stretch}", align_bytes=64)
-            x, c0 = [(raw[i], lo) for i, (pa, lo, hi) in enumerate(LOADS) if pa == a and lo <= t0 < hi][0]
+        grouped = [held.tile([P, t1 - t0, 4], BF16, name=f"grouped{i}", align_bytes=64) for i, (a, t0, t1) in enumerate(STRETCHES)]
+
+        def interleave(load):
+            a, c0, c1, on_vector = LOADS[load]
+            dst, t0 = [(grouped[i], lo) for i, (pa, lo, hi) in enumerate(STRETCHES) if pa == a and lo <= c0 < hi][0]
 
             def views(lo, hi):
                 return (
-                    grouped[:, lo:hi, :].rearrange("p (c i) j -> p c j i", i=2),
-                    x[:, :, t0 - c0 + lo : t0 - c0 + hi].rearrange("p j (c i) -> p c j i", i=2),
+                    dst[:, c0 - t0 + lo : c0 - t0 + hi, :].rearrange("p (c i) j -> p c j i", i=2),
+                    raw[load][:, :, lo:hi].rearrange("p j (c i) -> p c j i", i=2),
                 )
 
-            nc.scalar.copy(*views(on_vector, t1 - t0))
+            nc.scalar.copy(*views(on_vector, c1 - c0))
             if on_vector > 0:
                 nc.vector.tensor_copy(*views(0, on_vector))
-            return grouped
 
         def first_word(a):
             return (PASSES - 1 - a) * T
 
-        def quantize(stretch, grouped):
-            a, t0, t1 = STRETCHES[stretch][:3]
+        def quantize(stretch):
+            a, t0, t1 = STRETCHES[stretch]
             nc.vector.quantize_mx(
                 out=token_words[:, first_word(a) + t0 : first_word(a) + t1].bitcast(FP8X4),
                 scales=token_scale[:, T + t0 : T + t1] if a == 2 else token_scale[4 * a : P, t0:t1],
-                in_=grouped[:].rearrange("p w j -> p (w j)"),
+                in_=grouped[stretch][:].rearrange("p w j -> p (w j)"),
             )
 
         for a in range(PASSES):
-            stretches = [i for i in range(len(STRETCHES)) if STRETCHES[i][0] == a]
-            for stretch, grouped in zip(stretches, [interleave(i) for i in stretches]):
-                quantize(stretch, grouped)
+            for load in range(len(LOADS)):
+                if LOADS[load][0] == a:
+                    interleave(load)
+            for stretch in range(len(STRETCHES)):
+                if STRETCHES[stretch][0] == a:
+                    quantize(stretch)
             if a == 1:
                 gather(picked01, token_scale[:], 0, S)
                 nc.sync.dma_start(out=moved1[0:SHIFT_ROWS, :].bitcast(I32), in_=picked01[4 : 4 + SHIFT_ROWS, :].bitcast(I32))
-                load_weights(order[AHEAD_OF_SHIFT:])
-            if a < 2:
-                gather(slot_words[a], token_words[:, first_word(a) : first_word(a) + 2 * T], 0, S)
+                load_weights(weight_loads[AHEAD_OF_SHIFT : 2 * G])
+                nc.sync.dma_start(out=bias[:, :, 0:E], in_=b.rearrange("(h p) e -> p h e", p=P))
+                load_weights(weight_loads[2 * G :])
+            if a == 0:
+                gather(slot_words[0], token_words[:, first_word(0) :], 0, S // 2)
+                gather(slot_words[0], token_words[:, first_word(0) :], S // 2, S)
+            if a == 1:
+                gather(slot_words[1], token_words[:, first_word(1) :], 0, S)
 
         e0 = 0
         for e1 in LAST_PASS_ENDS:
@@ -122,20 +139,24 @@ def tile_moe_eps_lin_relu_kernel(tc, xT, w_words, w_scales, b, offs, out):
             gather(slot_words[2], token_words[:, 0:T], C * e0, C * e1)
             e0 = e1
 
-        sums = {}
+        paired = 2 * G
+        banks = [psum.tile([P, 2, 2, C], F32, name=f"pair{i}") for i in range(paired // 2)]
+        sums = [banks[e // 2][:, e % 2] for e in range(paired)]
+        sums.extend(psum.tile([P, 2, C], F32, name=f"single{e}")[:] for e in range(paired, E))
 
         def multiply(e, a):
-            if a == 0:
-                sums[e] = psum.tile([P, 2, C], F32, name="acc")
+            words = late[e // G][:, e % G] if a == 2 else early[e][:, a]
+            opens = e >= paired or e % 2 == 0
+            closes = e >= paired or e % 2 == 1
             for h in range(2):
                 nc.tensor.matmul_mx(
                     out=sums[e][:, h, :],
-                    lhsT=weights[e][a][:, 2 * P * h : 2 * P * (h + 1)].bitcast(FP4X4),
+                    lhsT=words[:, 2 * P * h : 2 * P * (h + 1)].bitcast(FP4X4),
                     lhsT_scale=w_scale[:, PASSES * e + a, P * h : P * (h + 1)],
                     rhs=slot_words[a][:, C * e : C * e + C].bitcast(FP8X4),
                     rhs_scale=(picked01, moved1, picked2)[a][:, C * e : C * e + C],
-                    start=(a == 0 and h == 0),
-                    stop=(a == PASSES - 1 and h == 1),
+                    start=(a == 0 and h == 0 and opens),
+                    stop=(a == PASSES - 1 and h == 1 and closes),
                 )
 
         def finish(e):
@@ -149,9 +170,19 @@ def tile_moe_eps_lin_relu_kernel(tc, xT, w_words, w_scales, b, offs, out):
         out_rows = out.rearrange("(h p) (m s) -> h p m s", p=P, m=RANKS)
         places = C // RANKS
         stored = 0
-        for e, a in order:
-            multiply(e, a)
-            if a == PASSES - 1:
+        for k, last in steps:
+            block = range(G * k, G * k + G)
+            if not last:
+                for a in range(2):
+                    for e in block:
+                        multiply(e, a)
+                continue
+            for e in block:
+                multiply(e, 2)
+                if e < paired and e % 2 == 0:
+                    continue
+                if e < paired:
+                    finish(e - 1)
                 finish(e)
                 if e + 1 in LAST_PASS_ENDS:
                     for h in range(2):

@@ -20,11 +20,11 @@ ADD = mybir.AluOpType.add
 MAX = mybir.AluOpType.max
 
 LOADS = (
-    (0, 0, 512, 320), (0, 512, 768, 0), (0, 768, 1024, 176),
+    (0, 0, 256, 128), (0, 256, 512, 176), (0, 512, 768, 0), (0, 768, 1024, 0),
     (1, 0, 256, 0), (1, 256, 512, 0), (1, 512, 768, 0), (1, 768, 1024, 160),
     (2, 0, 512, 0), (2, 512, 1024, 0),
 )
-STRETCHES = ((0, 0, 512), (0, 512, 768), (0, 768, 1024), (1, 0, 512), (1, 512, 768), (1, 768, 1024), (2, 0, 512), (2, 512, 1024))
+STRETCHES = ((0, 0, 256), (0, 256, 512), (0, 512, 768), (0, 768, 1024), (1, 0, 512), (1, 512, 768), (1, 768, 1024), (2, 0, 512), (2, 512, 1024))
 G = 4
 BLOCKS = E // G
 LAST_PASS_ENDS = (4, 8, 10, 12)
@@ -45,7 +45,7 @@ def tile_moe_eps_lin_relu_kernel(tc, xT, w_words, w_scales, b, offs, out):
         picked01 = held.tile([P, S], U8, name="picked01", align_bytes=64)
         moved1 = held.tile([P, S], U8, name="moved", align_bytes=64)
         picked2 = held.tile([P, S], U8, name="picked2", align_bytes=64)
-        token_words = held.tile([P, PASSES * T], U32, name="codes", align_bytes=64)
+        token_words = [held.tile([P, T], U32, name=f"codes{a}", align_bytes=64) for a in range(PASSES)]
         slot_words = [held.tile([P, S], U32, name=f"slots{a}", align_bytes=64) for a in range(PASSES)]
         results = held.tile([P, 2, RANKS, E, C // RANKS], F32, name="ot", align_bytes=64)
         early = [held.tile([P, 2, 2 * N], U8, name=f"early{e}", align_bytes=64) for e in range(E)]
@@ -59,7 +59,7 @@ def tile_moe_eps_lin_relu_kernel(tc, xT, w_words, w_scales, b, offs, out):
             x = held.tile([P, 4, c1 - c0], F32, name=f"raw{i}", align_bytes=64)
             nc.sync.dma_start(out=x[:], in_=xT[512 * a : 512 * a + 512, c0:c1].rearrange("(p j) w -> p j w", j=4))
             raw.append(x)
-            if c1 == T and a == 0:
+            if c1 == T // 2 and a == 0:
                 nc.sync.dma_start(offsets[:], offs)
 
         scale_rows = w_scales.bitcast(I32).rearrange("e a q n -> q (e a) n")
@@ -102,13 +102,10 @@ def tile_moe_eps_lin_relu_kernel(tc, xT, w_words, w_scales, b, offs, out):
             if on_vector > 0:
                 nc.vector.tensor_copy(*views(0, on_vector))
 
-        def first_word(a):
-            return (PASSES - 1 - a) * T
-
         def quantize(stretch):
             a, t0, t1 = STRETCHES[stretch]
             nc.vector.quantize_mx(
-                out=token_words[:, first_word(a) + t0 : first_word(a) + t1].bitcast(FP8X4),
+                out=token_words[a][:, t0:t1].bitcast(FP8X4),
                 scales=token_scale[:, T + t0 : T + t1] if a == 2 else token_scale[4 * a : P, t0:t1],
                 in_=grouped[stretch][:].rearrange("p w j -> p (w j)"),
             )
@@ -120,24 +117,25 @@ def tile_moe_eps_lin_relu_kernel(tc, xT, w_words, w_scales, b, offs, out):
             for stretch in range(len(STRETCHES)):
                 if STRETCHES[stretch][0] == a:
                     quantize(stretch)
+                    if a == 0 and STRETCHES[stretch][2] % (T // RANKS) == 0:
+                        end = STRETCHES[stretch][2]
+                        for e in range(E):
+                            s0 = C * e + (end // (T // RANKS) - 1) * (C // RANKS)
+                            gather(slot_words[0], token_words[0][:, 0:end], s0, s0 + C // RANKS)
             if a == 1:
                 gather(picked01, token_scale[:], 0, S)
                 nc.sync.dma_start(out=moved1[0:SHIFT_ROWS, :].bitcast(I32), in_=picked01[4 : 4 + SHIFT_ROWS, :].bitcast(I32))
                 load_weights(weight_loads[AHEAD_OF_SHIFT : 2 * G])
                 nc.sync.dma_start(out=bias[:, :, 0:E], in_=b.rearrange("(h p) e -> p h e", p=P))
                 load_weights(weight_loads[2 * G :])
-            if a == 0:
-                gather(slot_words[0], token_words[:, first_word(0) :], 0, S // 2)
-                gather(slot_words[0], token_words[:, first_word(0) :], S // 2, S)
             if a == 1:
-                gather(slot_words[1], token_words[:, first_word(1) :], 0, S)
+                gather(slot_words[1], token_words[1][:], 0, S // 2)
+                gather(slot_words[1], token_words[1][:], S // 2, S)
 
-        e0 = 0
-        for e1 in LAST_PASS_ENDS:
-            if e0 % G == 0:
-                gather(picked2, token_scale[:, T:], C * e0, C * (e0 + G))
-            gather(slot_words[2], token_words[:, 0:T], C * e0, C * e1)
-            e0 = e1
+        for bytes_from, bytes_to, word_ends in ((0, 4, (4,)), (4, 8, (8,)), (8, 10, (10,)), (10, 12, (11, 12))):
+            gather(picked2, token_scale[:, T:], C * bytes_from, C * bytes_to)
+            for e0, e1 in zip((bytes_from,) + word_ends, word_ends):
+                gather(slot_words[2], token_words[2][:], C * e0, C * e1)
 
         paired = 2 * G
         banks = [psum.tile([P, 2, 2, C], F32, name=f"pair{i}") for i in range(paired // 2)]

@@ -27,9 +27,10 @@ LOADS = (
 STRETCHES = ((0, 0, 256), (0, 256, 512), (0, 512, 768), (0, 768, 1024), (1, 0, 512), (1, 512, 768), (1, 768, 1024), (2, 0, 512), (2, 512, 1024))
 G = 4
 BLOCKS = E // G
-LAST_PASS_ENDS = (4, 8, 10, 12)
+STEPS = ((0, 0), (0, 1), (1, 0), (0, 2), (1, 1), (2, 0), (1, 2), (2, 1), (2, 2))
+LAST_GATHERS = ((0, 4, (4,)), (4, 8, (6, 8)), (8, 10, (10,)), (10, 12, (11, 12)))
+STORE_ENDS = (4, 8, 10, 12)
 SHIFT_ROWS = 112
-AHEAD_OF_SHIFT = 2
 
 
 def tile_moe_eps_lin_relu_kernel(tc, xT, w_words, w_scales, b, offs, out):
@@ -48,8 +49,7 @@ def tile_moe_eps_lin_relu_kernel(tc, xT, w_words, w_scales, b, offs, out):
         token_words = [held.tile([P, T], U32, name=f"codes{a}", align_bytes=64) for a in range(PASSES)]
         slot_words = [held.tile([P, S], U32, name=f"slots{a}", align_bytes=64) for a in range(PASSES)]
         results = held.tile([P, 2, RANKS, E, C // RANKS], F32, name="ot", align_bytes=64)
-        early = [held.tile([P, 2, 2 * N], U8, name=f"early{e}", align_bytes=64) for e in range(E)]
-        late = [held.tile([P, G, 2 * N], U8, name=f"late{k}", align_bytes=64) for k in range(BLOCKS)]
+        weights = {(k, a): held.tile([P, G, 2 * N], U8, name=f"weights{k}_{a}", align_bytes=64) for k, a in STEPS}
         nc.vector.memset(token_scale[:].bitcast(I32), 0)
         nc.vector.memset(w_scale[:].rearrange("p g n -> p (g n)").bitcast(I32), 0)
         nc.vector.memset(moved1[:].bitcast(I32), 0)
@@ -63,25 +63,15 @@ def tile_moe_eps_lin_relu_kernel(tc, xT, w_words, w_scales, b, offs, out):
                 nc.sync.dma_start(offsets[:], offs)
 
         scale_rows = w_scales.bitcast(I32).rearrange("e a q n -> q (e a) n")
-        for k in range(BLOCKS):
-            rows = slice(G * PASSES * k, G * PASSES * (k + 1))
-            for r in range(4):
-                nc.sync.dma_start(out=w_scale[r:P:32, rows, :].bitcast(I32), in_=scale_rows[r:16:4, rows, :])
+        for r in range(4):
+            nc.sync.dma_start(out=w_scale[r:P:32].bitcast(I32), in_=scale_rows[r:16:4])
 
-        weight_words = w_words.bitcast(I32)
-        steps = [(0, False), (1, False), (0, True), (2, False), (1, True), (2, True)]
-        weight_loads = []
-        for k, last in steps:
-            if last:
-                weight_loads.append((late[k], weight_words[G * k : G * k + G, 2].rearrange("e p n -> p e n")))
-            else:
-                weight_loads.extend((early[e], weight_words[e, 0:2].rearrange("a p n -> p a n")) for e in range(G * k, G * k + G))
+        def load_weights(steps):
+            for k, a in steps:
+                words = w_words.bitcast(I32)[G * k : G * k + G, a].rearrange("e p n -> p e n")
+                nc.sync.dma_start(out=weights[k, a][:].bitcast(I32), in_=words)
 
-        def load_weights(loads):
-            for tile, words in loads:
-                nc.sync.dma_start(out=tile[:].bitcast(I32), in_=words)
-
-        load_weights(weight_loads[:AHEAD_OF_SHIFT])
+        load_weights(STEPS[:1])
 
         def gather(dst, window, s0, s1):
             nc.vector.tensor_copy(dst[:, s0:s1], window.indirect(offsets[:, s0 // 16 : s1 // 16]))
@@ -125,14 +115,14 @@ def tile_moe_eps_lin_relu_kernel(tc, xT, w_words, w_scales, b, offs, out):
             if a == 1:
                 gather(picked01, token_scale[:], 0, S)
                 nc.sync.dma_start(out=moved1[0:SHIFT_ROWS, :].bitcast(I32), in_=picked01[4 : 4 + SHIFT_ROWS, :].bitcast(I32))
-                load_weights(weight_loads[AHEAD_OF_SHIFT : 2 * G])
+                load_weights(STEPS[1:3])
                 nc.sync.dma_start(out=bias[:, :, 0:E], in_=b.rearrange("(h p) e -> p h e", p=P))
-                load_weights(weight_loads[2 * G :])
+                load_weights(STEPS[3:])
             if a == 1:
                 gather(slot_words[1], token_words[1][:], 0, S // 2)
                 gather(slot_words[1], token_words[1][:], S // 2, S)
 
-        for bytes_from, bytes_to, word_ends in ((0, 4, (4,)), (4, 8, (8,)), (8, 10, (10,)), (10, 12, (11, 12))):
+        for bytes_from, bytes_to, word_ends in LAST_GATHERS:
             gather(picked2, token_scale[:, T:], C * bytes_from, C * bytes_to)
             for e0, e1 in zip((bytes_from,) + word_ends, word_ends):
                 gather(slot_words[2], token_words[2][:], C * e0, C * e1)
@@ -143,7 +133,7 @@ def tile_moe_eps_lin_relu_kernel(tc, xT, w_words, w_scales, b, offs, out):
         sums.extend(psum.tile([P, 2, C], F32, name=f"single{e}")[:] for e in range(paired, E))
 
         def multiply(e, a):
-            words = late[e // G][:, e % G] if a == 2 else early[e][:, a]
+            words = weights[e // G, a][:, e % G]
             opens = e >= paired or e % 2 == 0
             closes = e >= paired or e % 2 == 1
             for h in range(2):
@@ -168,21 +158,15 @@ def tile_moe_eps_lin_relu_kernel(tc, xT, w_words, w_scales, b, offs, out):
         out_rows = out.rearrange("(h p) (m s) -> h p m s", p=P, m=RANKS)
         places = C // RANKS
         stored = 0
-        for k, last in steps:
-            block = range(G * k, G * k + G)
-            if not last:
-                for a in range(2):
-                    for e in block:
-                        multiply(e, a)
-                continue
-            for e in block:
-                multiply(e, 2)
-                if e < paired and e % 2 == 0:
+        for k, a in STEPS:
+            for e in range(G * k, G * k + G):
+                multiply(e, a)
+                if a < 2 or (e < paired and e % 2 == 0):
                     continue
                 if e < paired:
                     finish(e - 1)
                 finish(e)
-                if e + 1 in LAST_PASS_ENDS:
+                if e + 1 in STORE_ENDS:
                     for h in range(2):
                         nc.sync.dma_start(
                             out=out_rows[h, :, :, places * stored : places * (e + 1)],

@@ -20,15 +20,15 @@ ADD = mybir.AluOpType.add
 MAX = mybir.AluOpType.max
 
 LOADS = (
-    (0, 0, 256, 128), (0, 256, 512, 176), (0, 512, 768, 0), (0, 768, 1024, 0),
-    (1, 0, 256, 0), (1, 256, 512, 0), (1, 512, 768, 0), (1, 768, 1024, 160),
+    (0, 0, 512, 320), (0, 512, 768, 0), (0, 768, 1024, 144),
+    (1, 0, 256, 0), (1, 256, 512, 0), (1, 512, 768, 0), (1, 768, 1024, 128),
     (2, 0, 512, 0), (2, 512, 1024, 0),
 )
-STRETCHES = ((0, 0, 256), (0, 256, 512), (0, 512, 768), (0, 768, 1024), (1, 0, 512), (1, 512, 768), (1, 768, 1024), (2, 0, 512), (2, 512, 1024))
+STRETCHES = ((0, 0, 512), (0, 512, 768), (0, 768, 1024), (1, 0, 512), (1, 512, 768), (1, 768, 1024), (2, 0, 1024))
 G = 4
 BLOCKS = E // G
 STEPS = ((0, 0), (0, 1), (1, 0), (0, 2), (1, 1), (2, 0), (1, 2), (2, 1), (2, 2))
-LAST_GATHERS = ((0, 4, (4,)), (4, 8, (6, 8)), (8, 10, (10,)), (10, 12, (11, 12)))
+LAST_GATHERS = ((0, 4, (4,)), (4, 8, (8,)), (8, 12, (10, 12)))
 STORE_ENDS = (4, 8, 10, 12)
 SHIFT_ROWS = 112
 
@@ -46,8 +46,8 @@ def tile_moe_eps_lin_relu_kernel(tc, xT, w_words, w_scales, b, offs, out):
         picked01 = held.tile([P, S], U8, name="picked01", align_bytes=64)
         moved1 = held.tile([P, S], U8, name="moved", align_bytes=64)
         picked2 = held.tile([P, S], U8, name="picked2", align_bytes=64)
-        token_words = [held.tile([P, T], U32, name=f"codes{a}", align_bytes=64) for a in range(PASSES)]
-        slot_words = [held.tile([P, S], U32, name=f"slots{a}", align_bytes=64) for a in range(PASSES)]
+        token_words = held.tile([P, PASSES * T], U32, name="codes", align_bytes=64)
+        slot_words = [held.tile([P, S if a == 2 else S - C], U32, name=f"slots{a}", align_bytes=64) for a in range(PASSES)]
         results = held.tile([P, 2, RANKS, E, C // RANKS], F32, name="ot", align_bytes=64)
         weights = {(k, a): held.tile([P, G, 2 * N], U8, name=f"weights{k}_{a}", align_bytes=64) for k, a in STEPS}
         nc.vector.memset(token_scale[:].bitcast(I32), 0)
@@ -59,7 +59,7 @@ def tile_moe_eps_lin_relu_kernel(tc, xT, w_words, w_scales, b, offs, out):
             x = held.tile([P, 4, c1 - c0], F32, name=f"raw{i}", align_bytes=64)
             nc.sync.dma_start(out=x[:], in_=xT[512 * a : 512 * a + 512, c0:c1].rearrange("(p j) w -> p j w", j=4))
             raw.append(x)
-            if c1 == T // 2 and a == 0:
+            if c1 == T and a == 0:
                 nc.sync.dma_start(offsets[:], offs)
 
         scale_rows = w_scales.bitcast(I32).rearrange("e a q n -> q (e a) n")
@@ -73,8 +73,9 @@ def tile_moe_eps_lin_relu_kernel(tc, xT, w_words, w_scales, b, offs, out):
 
         load_weights(STEPS[:1])
 
-        def gather(dst, window, s0, s1):
-            nc.vector.tensor_copy(dst[:, s0:s1], window.indirect(offsets[:, s0 // 16 : s1 // 16]))
+        def gather(dst, window, s0, s1, d0=None):
+            d0 = s0 if d0 is None else d0
+            nc.vector.tensor_copy(dst[:, d0 : d0 + s1 - s0], window.indirect(offsets[:, s0 // 16 : s1 // 16]))
 
         grouped = [held.tile([P, t1 - t0, 4], BF16, name=f"grouped{i}", align_bytes=64) for i, (a, t0, t1) in enumerate(STRETCHES)]
 
@@ -92,14 +93,19 @@ def tile_moe_eps_lin_relu_kernel(tc, xT, w_words, w_scales, b, offs, out):
             if on_vector > 0:
                 nc.vector.tensor_copy(*views(0, on_vector))
 
+        def words_of(a, columns):
+            first = (PASSES - 1 - a) * T
+            return token_words[:, first : first + columns]
+
         def quantize(stretch):
             a, t0, t1 = STRETCHES[stretch]
             nc.vector.quantize_mx(
-                out=token_words[a][:, t0:t1].bitcast(FP8X4),
+                out=words_of(a, T)[:, t0:t1].bitcast(FP8X4),
                 scales=token_scale[:, T + t0 : T + t1] if a == 2 else token_scale[4 * a : P, t0:t1],
                 in_=grouped[stretch][:].rearrange("p w j -> p (w j)"),
             )
 
+        last_words = []
         for a in range(PASSES):
             for load in range(len(LOADS)):
                 if LOADS[load][0] == a:
@@ -107,11 +113,14 @@ def tile_moe_eps_lin_relu_kernel(tc, xT, w_words, w_scales, b, offs, out):
             for stretch in range(len(STRETCHES)):
                 if STRETCHES[stretch][0] == a:
                     quantize(stretch)
-                    if a == 0 and STRETCHES[stretch][2] % (T // RANKS) == 0:
-                        end = STRETCHES[stretch][2]
-                        for e in range(E):
-                            s0 = C * e + (end // (T // RANKS) - 1) * (C // RANKS)
-                            gather(slot_words[0], token_words[0][:, 0:end], s0, s0 + C // RANKS)
+            if a > 0:
+                last_load = [i for i in range(len(LOADS)) if LOADS[i][0] == a][-1]
+                tile = held.tile([P, C], U32, name=f"last_words{a - 1}", tag=f"raw{last_load}", align_bytes=64)
+                last_words.append(tile)
+                gather(tile, words_of(a - 1, T), S - C, S, 0)
+            if a == 0:
+                gather(slot_words[0], words_of(0, T), 0, (S - C) // 2)
+                gather(slot_words[0], words_of(0, T), (S - C) // 2, S - C)
             if a == 1:
                 gather(picked01, token_scale[:], 0, S)
                 nc.sync.dma_start(out=moved1[0:SHIFT_ROWS, :].bitcast(I32), in_=picked01[4 : 4 + SHIFT_ROWS, :].bitcast(I32))
@@ -119,13 +128,12 @@ def tile_moe_eps_lin_relu_kernel(tc, xT, w_words, w_scales, b, offs, out):
                 nc.sync.dma_start(out=bias[:, :, 0:E], in_=b.rearrange("(h p) e -> p h e", p=P))
                 load_weights(STEPS[3:])
             if a == 1:
-                gather(slot_words[1], token_words[1][:], 0, S // 2)
-                gather(slot_words[1], token_words[1][:], S // 2, S)
+                gather(slot_words[1], words_of(1, 2 * T), 0, S - C)
 
         for bytes_from, bytes_to, word_ends in LAST_GATHERS:
             gather(picked2, token_scale[:, T:], C * bytes_from, C * bytes_to)
             for e0, e1 in zip((bytes_from,) + word_ends, word_ends):
-                gather(slot_words[2], token_words[2][:], C * e0, C * e1)
+                gather(slot_words[2], words_of(2, T), C * e0, C * e1)
 
         paired = 2 * G
         banks = [psum.tile([P, 2, 2, C], F32, name=f"pair{i}") for i in range(paired // 2)]
@@ -141,7 +149,7 @@ def tile_moe_eps_lin_relu_kernel(tc, xT, w_words, w_scales, b, offs, out):
                     out=sums[e][:, h, :],
                     lhsT=words[:, 2 * P * h : 2 * P * (h + 1)].bitcast(FP4X4),
                     lhsT_scale=w_scale[:, PASSES * e + a, P * h : P * (h + 1)],
-                    rhs=slot_words[a][:, C * e : C * e + C].bitcast(FP8X4),
+                    rhs=(last_words[a][:] if e == E - 1 and a < 2 else slot_words[a][:, C * e : C * e + C]).bitcast(FP8X4),
                     rhs_scale=(picked01, moved1, picked2)[a][:, C * e : C * e + C],
                     start=(a == 0 and h == 0 and opens),
                     stop=(a == PASSES - 1 and h == 1 and closes),

@@ -25,11 +25,10 @@ LOADS = (
     (2, 0, 512, 0), (2, 512, 1024, 0),
 )
 STRETCHES = ((0, 0, 512), (0, 512, 768), (0, 768, 1024), (1, 0, 512), (1, 512, 768), (1, 768, 1024), (2, 0, 1024))
-G = 4
-BLOCKS = E // G
-STEPS = ((0, 0), (0, 1), (1, 0), (0, 2), (1, 1), (2, 0), (1, 2), (2, 1), (2, 2))
+STEPS = ((0, 4, 0), (0, 4, 1), (4, 8, 0), (0, 4, 2), (4, 8, 1), (8, 12, 0), (4, 8, 2), (8, 12, 1), (8, 10, 2), (10, 12, 2))
 LAST_GATHERS = ((0, 4, (4,)), (4, 8, (8,)), (8, 12, (10, 12)))
-STORE_ENDS = (4, 8, 10, 12)
+STORE_ENDS = (4, 8, 12)
+PAIRED = 8
 SHIFT_ROWS = 112
 
 
@@ -49,7 +48,6 @@ def tile_moe_eps_lin_relu_kernel(tc, xT, w_words, w_scales, b, offs, out):
         token_words = held.tile([P, PASSES * T], U32, name="codes", align_bytes=64)
         slot_words = [held.tile([P, S if a == 2 else S - C], U32, name=f"slots{a}", align_bytes=64) for a in range(PASSES)]
         results = held.tile([P, 2, RANKS, E, C // RANKS], F32, name="ot", align_bytes=64)
-        weights = {(k, a): held.tile([P, G, 2 * N], U8, name=f"weights{k}_{a}", align_bytes=64) for k, a in STEPS}
         nc.vector.memset(token_scale[:].bitcast(I32), 0)
         nc.vector.memset(w_scale[:].rearrange("p g n -> p (g n)").bitcast(I32), 0)
         nc.vector.memset(moved1[:].bitcast(I32), 0)
@@ -66,16 +64,19 @@ def tile_moe_eps_lin_relu_kernel(tc, xT, w_words, w_scales, b, offs, out):
         for r in range(4):
             nc.sync.dma_start(out=w_scale[r:P:32].bitcast(I32), in_=scale_rows[r:16:4])
 
+        weights = {}
+
         def load_weights(steps):
-            for k, a in steps:
-                words = w_words.bitcast(I32)[G * k : G * k + G, a].rearrange("e p n -> p e n")
-                nc.sync.dma_start(out=weights[k, a][:].bitcast(I32), in_=words)
+            for e0, e1, a in steps:
+                tile = held.tile([P, e1 - e0, 2 * N], U8, name=f"weights{e0}_{a}", align_bytes=64)
+                nc.sync.dma_start(out=tile[:].bitcast(I32), in_=w_words.bitcast(I32)[e0:e1, a].rearrange("e p n -> p e n"))
+                for e in range(e0, e1):
+                    weights[e, a] = tile[:, e - e0]
 
         load_weights(STEPS[:1])
 
-        def gather(dst, window, s0, s1, d0=None):
-            d0 = s0 if d0 is None else d0
-            nc.vector.tensor_copy(dst[:, d0 : d0 + s1 - s0], window.indirect(offsets[:, s0 // 16 : s1 // 16]))
+        def gather(dst, window, s0, s1):
+            nc.vector.tensor_copy(dst, window.indirect(offsets[:, s0 // 16 : s1 // 16]))
 
         grouped = [held.tile([P, t1 - t0, 4], BF16, name=f"grouped{i}", align_bytes=64) for i, (a, t0, t1) in enumerate(STRETCHES)]
 
@@ -117,33 +118,32 @@ def tile_moe_eps_lin_relu_kernel(tc, xT, w_words, w_scales, b, offs, out):
                 last_load = [i for i in range(len(LOADS)) if LOADS[i][0] == a][-1]
                 tile = held.tile([P, C], U32, name=f"last_words{a - 1}", tag=f"raw{last_load}", align_bytes=64)
                 last_words.append(tile)
-                gather(tile, words_of(a - 1, T), S - C, S, 0)
+                gather(tile[:], words_of(a - 1, T), S - C, S)
             if a == 0:
-                gather(slot_words[0], words_of(0, T), 0, (S - C) // 2)
-                gather(slot_words[0], words_of(0, T), (S - C) // 2, S - C)
+                half = (S - C) // 2
+                gather(slot_words[0][:, 0:half], words_of(0, T), 0, half)
+                gather(slot_words[0][:, half:], words_of(0, T), half, S - C)
             if a == 1:
-                gather(picked01, token_scale[:], 0, S)
+                gather(picked01[:], token_scale[:], 0, S)
                 nc.sync.dma_start(out=moved1[0:SHIFT_ROWS, :].bitcast(I32), in_=picked01[4 : 4 + SHIFT_ROWS, :].bitcast(I32))
                 load_weights(STEPS[1:3])
                 nc.sync.dma_start(out=bias[:, :, 0:E], in_=b.rearrange("(h p) e -> p h e", p=P))
                 load_weights(STEPS[3:])
-            if a == 1:
-                gather(slot_words[1], words_of(1, 2 * T), 0, S - C)
+                gather(slot_words[1][:], words_of(1, 2 * T), 0, S - C)
 
         for bytes_from, bytes_to, word_ends in LAST_GATHERS:
-            gather(picked2, token_scale[:, T:], C * bytes_from, C * bytes_to)
+            gather(picked2[:, C * bytes_from : C * bytes_to], token_scale[:, T:], C * bytes_from, C * bytes_to)
             for e0, e1 in zip((bytes_from,) + word_ends, word_ends):
-                gather(slot_words[2], words_of(2, T), C * e0, C * e1)
+                gather(slot_words[2][:, C * e0 : C * e1], words_of(2, T), C * e0, C * e1)
 
-        paired = 2 * G
-        banks = [psum.tile([P, 2, 2, C], F32, name=f"pair{i}") for i in range(paired // 2)]
-        sums = [banks[e // 2][:, e % 2] for e in range(paired)]
-        sums.extend(psum.tile([P, 2, C], F32, name=f"single{e}")[:] for e in range(paired, E))
+        banks = [psum.tile([P, 2, 2, C], F32, name=f"pair{i}") for i in range(PAIRED // 2)]
+        sums = [banks[e // 2][:, e % 2] for e in range(PAIRED)]
+        sums.extend(psum.tile([P, 2, C], F32, name=f"single{e}")[:] for e in range(PAIRED, E))
 
         def multiply(e, a):
-            words = weights[e // G, a][:, e % G]
-            opens = e >= paired or e % 2 == 0
-            closes = e >= paired or e % 2 == 1
+            words = weights[e, a]
+            opens = e >= PAIRED or e % 2 == 0
+            closes = e >= PAIRED or e % 2 == 1
             for h in range(2):
                 nc.tensor.matmul_mx(
                     out=sums[e][:, h, :],
@@ -166,12 +166,12 @@ def tile_moe_eps_lin_relu_kernel(tc, xT, w_words, w_scales, b, offs, out):
         out_rows = out.rearrange("(h p) (m s) -> h p m s", p=P, m=RANKS)
         places = C // RANKS
         stored = 0
-        for k, a in STEPS:
-            for e in range(G * k, G * k + G):
+        for e0, e1, a in STEPS:
+            for e in range(e0, e1):
                 multiply(e, a)
-                if a < 2 or (e < paired and e % 2 == 0):
+                if a < 2 or (e < PAIRED and e % 2 == 0):
                     continue
-                if e < paired:
+                if e < PAIRED:
                     finish(e - 1)
                 finish(e)
                 if e + 1 in STORE_ENDS:

@@ -86,8 +86,8 @@ def tile_moe_eps_lin_relu_kernel(tc, xT, w_words, w_scales, b, offs, out):
 
             def views(lo, hi):
                 return (
-                    dst[:, c0 - t0 + lo : c0 - t0 + hi, :].rearrange("p (c i) j -> p c j i", i=2),
-                    raw[load][:, :, lo:hi].rearrange("p j (c i) -> p c j i", i=2),
+                    dst[:, c0 - t0 + lo : c0 - t0 + hi, :].rearrange("p (c i) j -> p c j i", i=4),
+                    raw[load][:, :, lo:hi].rearrange("p j (c i) -> p c j i", i=4),
                 )
 
             nc.scalar.copy(*views(on_vector, c1 - c0))

import concourse.mybir as mybir

FLOPS = 2 * 1536 * 1536 * 256

T, E, C, N = 1024, 12, 128, 256
P = 128
PASSES = 3
S = E * C
RANKS = 2
F32 = mybir.dt.float32
BF16 = mybir.dt.bfloat16
I32 = mybir.dt.int32
U32 = mybir.dt.uint32
U16 = mybir.dt.uint16
U8 = mybir.dt.uint8
FP8X4 = mybir.dt.float8_e4m3fn_x4
FP4X4 = mybir.dt.float4_e2m1fn_x4
RELU = mybir.ActivationFunctionType.Relu
ADD = mybir.AluOpType.add
MAX = mybir.AluOpType.max

LOADS = (
    (0, 0, 512, 320), (0, 512, 768, 0), (0, 768, 1024, 144),
    (1, 0, 256, 0), (1, 256, 512, 0), (1, 512, 768, 0), (1, 768, 1024, 128),
    (2, 0, 512, 0), (2, 512, 1024, 0),
)
STRETCHES = ((0, 0, 512), (0, 512, 768), (0, 768, 1024), (1, 0, 512), (1, 512, 768), (1, 768, 1024), (2, 0, 1024))
STEPS = ((0, 4, 0), (0, 4, 1), (4, 8, 0), (0, 4, 2), (4, 8, 1), (8, 12, 0), (4, 8, 2), (8, 12, 1), (8, 10, 2), (10, 12, 2))
LAST_GATHERS = ((0, 4, (4,)), (4, 8, (8,)), (8, 12, (10, 12)))
STORE_ENDS = (4, 8, 12)
PAIRED = 8
SHIFT_ROWS = 112


def tile_moe_eps_lin_relu_kernel(tc, xT, w_words, w_scales, b, offs, out):
    nc = tc.nc
    with (
        tc.tile_pool(name="held", bufs=1) as held,
        tc.psum_pool(name="psum", bufs=1) as psum,
    ):
        offsets = held.tile([P, S // 16], U16, name="offsets")
        bias = held.tile([P, 2, 16], F32, name="bias", align_bytes=64)
        w_scale = held.tile([P, E * PASSES, N], U8, name="ws", align_bytes=64)
        token_scale = held.tile([P, 2 * T], U8, name="planes", align_bytes=64)
        picked01 = held.tile([P, S], U8, name="picked01", align_bytes=64)
        moved1 = held.tile([P, S], U8, name="moved", align_bytes=64)
        picked2 = held.tile([P, S], U8, name="picked2", align_bytes=64)
        token_words = held.tile([P, PASSES * T], U32, name="codes", align_bytes=64)
        slot_words = [held.tile([P, S if a == 2 else S - C], U32, name=f"slots{a}", align_bytes=64) for a in range(PASSES)]
        results = held.tile([P, 2, RANKS, E, C // RANKS], F32, name="ot", align_bytes=64)
        nc.vector.memset(token_scale[:].bitcast(I32), 0)
        nc.vector.memset(w_scale[:].rearrange("p g n -> p (g n)").bitcast(I32), 0)
        nc.vector.memset(moved1[:].bitcast(I32), 0)

        raw = []
        for i, (a, c0, c1, on_vector) in enumerate(LOADS):
            x = held.tile([P, 4, c1 - c0], F32, name=f"raw{i}", align_bytes=64)
            nc.sync.dma_start(out=x[:], in_=xT[512 * a : 512 * a + 512, c0:c1].rearrange("(p j) w -> p j w", j=4))
            raw.append(x)
            if c1 == T and a == 0:
                nc.sync.dma_start(offsets[:], offs)

        scale_rows = w_scales.bitcast(I32).rearrange("e a q n -> q (e a) n")
        for r in range(4):
            nc.sync.dma_start(out=w_scale[r:P:32].bitcast(I32), in_=scale_rows[r:16:4])

        weights = {}

        def load_weights(steps):
            for e0, e1, a in steps:
                tile = held.tile([P, e1 - e0, 2 * N], U8, name=f"weights{e0}_{a}", align_bytes=64)
                nc.sync.dma_start(out=tile[:].bitcast(I32), in_=w_words.bitcast(I32)[e0:e1, a].rearrange("e p n -> p e n"))
                for e in range(e0, e1):
                    weights[e, a] = tile[:, e - e0]

        load_weights(STEPS[:1])

        def gather(dst, window, s0, s1):
            nc.vector.tensor_copy(dst, window.indirect(offsets[:, s0 // 16 : s1 // 16]))

        grouped = [held.tile([P, t1 - t0, 4], BF16, name=f"grouped{i}", align_bytes=64) for i, (a, t0, t1) in enumerate(STRETCHES)]

        def interleave(load):
            a, c0, c1, on_vector = LOADS[load]
            dst, t0 = [(grouped[i], lo) for i, (pa, lo, hi) in enumerate(STRETCHES) if pa == a and lo <= c0 < hi][0]

            def views(lo, hi):
                return (
                    dst[:, c0 - t0 + lo : c0 - t0 + hi, :].rearrange("p (c i) j -> p c j i", i=4),
                    raw[load][:, :, lo:hi].rearrange("p j (c i) -> p c j i", i=4),
                )

            nc.scalar.copy(*views(on_vector, c1 - c0))
            if on_vector > 0:
                nc.vector.tensor_copy(*views(0, on_vector))

        def words_of(a, columns):
            first = (PASSES - 1 - a) * T
            return token_words[:, first : first + columns]

        def quantize(stretch):
            a, t0, t1 = STRETCHES[stretch]
            nc.vector.quantize_mx(
                out=words_of(a, T)[:, t0:t1].bitcast(FP8X4),
                scales=token_scale[:, T + t0 : T + t1] if a == 2 else token_scale[4 * a : P, t0:t1],
                in_=grouped[stretch][:].rearrange("p w j -> p (w j)"),
            )

        last_words = []
        for a in range(PASSES):
            for load in range(len(LOADS)):
                if LOADS[load][0] == a:
                    interleave(load)
            for stretch in range(len(STRETCHES)):
                if STRETCHES[stretch][0] == a:
                    quantize(stretch)
            if a > 0:
                last_load = [i for i in range(len(LOADS)) if LOADS[i][0] == a][-1]
                tile = held.tile([P, C], U32, name=f"last_words{a - 1}", tag=f"raw{last_load}", align_bytes=64)
                last_words.append(tile)
                gather(tile[:], words_of(a - 1, T), S - C, S)
            if a == 0:
                half = (S - C) // 2
                gather(slot_words[0][:, 0:half], words_of(0, T), 0, half)
                gather(slot_words[0][:, half:], words_of(0, T), half, S - C)
            if a == 1:
                gather(picked01[:], token_scale[:], 0, S)
                nc.sync.dma_start(out=moved1[0:SHIFT_ROWS, :].bitcast(I32), in_=picked01[4 : 4 + SHIFT_ROWS, :].bitcast(I32))
                load_weights(STEPS[1:3])
                nc.sync.dma_start(out=bias[:, :, 0:E], in_=b.rearrange("(h p) e -> p h e", p=P))
                load_weights(STEPS[3:])
                gather(slot_words[1][:], words_of(1, 2 * T), 0, S - C)

        for bytes_from, bytes_to, word_ends in LAST_GATHERS:
            gather(picked2[:, C * bytes_from : C * bytes_to], token_scale[:, T:], C * bytes_from, C * bytes_to)
            for e0, e1 in zip((bytes_from,) + word_ends, word_ends):
                gather(slot_words[2][:, C * e0 : C * e1], words_of(2, T), C * e0, C * e1)

        banks = [psum.tile([P, 2, 2, C], F32, name=f"pair{i}") for i in range(PAIRED // 2)]
        sums = [banks[e // 2][:, e % 2] for e in range(PAIRED)]
        sums.extend(psum.tile([P, 2, C], F32, name=f"single{e}")[:] for e in range(PAIRED, E))

        def multiply(e, a):
            words = weights[e, a]
            opens = e >= PAIRED or e % 2 == 0
            closes = e >= PAIRED or e % 2 == 1
            for h in range(2):
                nc.tensor.matmul_mx(
                    out=sums[e][:, h, :],
                    lhsT=words[:, 2 * P * h : 2 * P * (h + 1)].bitcast(FP4X4),
                    lhsT_scale=w_scale[:, PASSES * e + a, P * h : P * (h + 1)],
                    rhs=(last_words[a][:] if e == E - 1 and a < 2 else slot_words[a][:, C * e : C * e + C]).bitcast(FP8X4),
                    rhs_scale=(picked01, moved1, picked2)[a][:, C * e : C * e + C],
                    start=(a == 0 and h == 0 and opens),
                    stop=(a == PASSES - 1 and h == 1 and closes),
                )

        def finish(e):
            for h in range(2):
                res, acc = results[:, h, :, e, :], sums[e][:, h, :].rearrange("p (m u) -> p m u", m=RANKS)
                if e == E - 1:
                    nc.vector.tensor_scalar(res, acc, bias[:, h, e : e + 1], 0.0, ADD, MAX)
                else:
                    nc.scalar.activation(out=res, in_=acc, func=RELU, bias=bias[:, h, e : e + 1])

        out_rows = out.rearrange("(h p) (m s) -> h p m s", p=P, m=RANKS)
        places = C // RANKS
        stored = 0
        for e0, e1, a in STEPS:
            for e in range(e0, e1):
                multiply(e, a)
                if a < 2 or (e < PAIRED and e % 2 == 0):
                    continue
                if e < PAIRED:
                    finish(e - 1)
                finish(e)
                if e + 1 in STORE_ENDS:
                    for h in range(2):
                        nc.sync.dma_start(
                            out=out_rows[h, :, :, places * stored : places * (e + 1)],
                            in_=results[:, h, :, stored : e + 1, :].rearrange("p m e u -> p m (e u)"),
                        )
                    stored = e + 1
